import numpy as np, ml_dtypes
CORES = [40,64,80,88,96,104,120,144]
N = 8
BF = ml_dtypes.bfloat16
def gentries(a):
    return np.ascontiguousarray(a.reshape(8, 16, -1).transpose(0, 2, 1)).reshape(8, -1)
def gtable(e):
    e = np.asarray(e); return np.ascontiguousarray(e.reshape(8, -1, 16).transpose(0, 2, 1)).reshape(128, -1).astype(np.int32)
FR, PR, MS, M, NT, KR, H, S = 2, 4, 1024, 4096, 1024, 4, 256, 10
C = 64
SIZES = ((24, 0), (48, 0), (80, 0), (128, 8), (192, 16), (320, 24), (640, 24), (NT, 24))
def sign(rng, shape):
    return 2 * rng.integers(0, 2, shape) - 1
def far(rng, shape):
    return rng.integers(244, 257, shape)
def scene(rng, size, w):
    pm = np.argsort(rng.random((8, M)), axis=1); inv = np.argsort(pm, axis=1); cl = pm % C
    cen = np.rint(rng.integers(16, 241, (8, 16, C)) * size)
    z = np.take_along_axis(cen, cl[:, None, :], 2)[None] + np.rint((2 * rng.random((FR, 8, 16, M)) - 1) * w)
    n0 = rng.integers(0, M, (8, NT)); c0 = np.take_along_axis(cl, n0, 1)
    x0 = np.take_along_axis(cen, c0[:, None, :], 2) + np.rint((2 * rng.random((8, 16, NT)) - 1) * rng.choice(np.array([16.0, 32.0, 48.0]), (8, 1, NT)))
    j = ((M // C) * rng.random((FR, 8, 3, M)) ** 3).astype(np.int64)
    same = inv[np.arange(8)[None, :, None, None], cl[None, :, None, :] + C * j]
    nx = np.where(rng.random((FR, 8, 3, M)) < np.array([0.6, 0.3, 0.3])[:, None], same, rng.integers(0, M, (FR, 8, 3, M)))
    nx[:, :, 1] = np.where(rng.random((FR, 8, M)) < 0.03125, nx[:, :, 0], nx[:, :, 1])
    return {"z": z, "nx": nx, "x0": x0, "n0": n0}
def folk(rng, s):
    return rng.permutation(NT)[:s][(s * rng.random((N, KR, H)) ** 1.5).astype(np.int64)]
def life(rng, d):
    o = rng.permutation(8); d["hy"] = np.zeros((N, 8, KR, H), np.int64); d["u"] = np.zeros((N, 8, FR, KR, H), np.int64)
    for g in range(8):
        s, lo = SIZES[int(o[g])]; d["hy"][:, g] = folk(rng, s); d["u"][:, g] = rng.integers(lo, 64, (N, FR, KR, H))
    return d
def plain(rng):
    return life(rng, scene(rng, np.ones((8, 1, C)), rng.choice(np.array([16.0, 32.0, 48.0, 64.0, 80.0]), (FR, 8, 1, M))))
def deal(rng, s):
    f = rng.permutation(N * H).reshape(N, 1, H) * KR + np.arange(KR)[:, None]
    return rng.permutation(NT)[:s][f % s], f // s
def quad(rng, d, g, near):
    b = rng.permutation(M // 4)[:NT]; d["n0"][g] = 4 * b
    x = rng.integers(32, 129, (16, NT)); d["x0"][g] = x
    for m in range(3): d["nx"][:, g, m] = 4 * (np.arange(M) // 4) + m + 1
    zz = d["z"][:, g]; zz[:] = far(rng, zz.shape)
    safe = np.argsort(rng.random((16, NT)), axis=0) < (16 if near == 3 else rng.integers(5, 17, (1, NT)))
    for m in range(1, near + 1):
        zz[:, :, 4 * b + m] = x + np.where(safe, rng.integers(-16, 17, (FR, 16, NT)), rng.integers(-72, 73, (FR, 16, NT)))
def soft(rng, d):
    q = int(rng.integers(0, N)); e = 3 * KR; k = np.arange(KR)[:, None]
    for g in range(8):
        c = rng.permutation(M)[:e]
        near = np.argsort(rng.random((16, e)), axis=0) < 5; near[:, :KR] = True
        x = np.where(near, rng.integers(96, 161, (16, e)), rng.integers(224, 257, (16, e))).astype(np.float64)
        step = np.full((16, e), 32.0); step[:, :KR] = 4.0 * (1 + rng.permutation(16) % 7)[:, None]
        d["x0"][g][:, :e] = x; d["n0"][g][:e] = c; d["nx"][:, g][:, :, c] = c
        for t in range(FR):
            v = np.where(near, x + sign(rng, (16, e)) * step, np.where(x >= 132, 8.0, 256.0))
            d["z"][t, g][:, c] = v; x = x + 0.25 * (v - x)
        o = rng.permutation(H)[H // 32:]; few = o[:H // 128]
        d["hy"][q, g][:, o] = KR + 2 * k + rng.integers(0, 2, (KR, len(o))); d["hy"][q, g][:, few] = k
        d["u"][q, g][:, :, o] = 63
def pack(d):
    z = np.clip(d["z"], 8, 256) * 0.03125; x = (np.clip(d["x0"], 8, 256) * 0.03125).reshape(1, 128, NT)
    z = np.ascontiguousarray(z.reshape(FR, 8, 16, PR, MS).transpose(0, 3, 1, 2, 4)).reshape(N, 128, MS)
    s = np.ascontiguousarray(d["nx"].reshape(FR, 8, 3, PR, MS).transpose(0, 3, 1, 2, 4)).reshape(N, 24, MS)
    return {"z": z.astype(np.float32).astype(BF), "nx": s.astype(np.int32), "x0": np.ascontiguousarray(np.repeat(x, N, axis=0)).astype(np.float32),
            "n0": np.ascontiguousarray(np.repeat(d["n0"][None], N, axis=0)).astype(np.int32),
            "hyp": np.stack([gtable(a.reshape(8, -1)) for a in d["hy"]]), "uu": np.stack([gtable(a.reshape(8, -1)) for a in d["u"]])}
def setup_inputs(rng):
    return pack(plain(rng))
def setup_inputs_spread(rng):
    d = life(rng, scene(rng, rng.choice(np.array([0.5, 0.75, 1.0, 1.25]), (8, 1, C)), 40 * np.exp2(2 * rng.random((FR, 8, 1, M)) - 1)))
    v = (64 * rng.random(d["u"].shape) ** rng.choice(np.array([0.5, 1.0, 2.0]), (1, 8, 1, 1, 1))).astype(np.int64)
    d["u"] = np.where(rng.random(v.shape) < 0.25, v, d["u"])
    soft(rng, d)
    return pack(d)
def atends(rng, a, hi, share):
    return np.where(rng.random(a.shape) < share, hi * rng.integers(0, 2, a.shape), a)
def setup_inputs_ends(rng):
    d = plain(rng); v = sign(rng, (8, 16, 1)); p = np.array([0.0, 0.0, 0.1, 0.3])
    sz = v[None] * sign(rng, (FR, 8, 1, M)) * np.where(rng.random((FR, 8, 16, M)) < rng.choice(p, (FR, 8, 1, M)), -1, 1)
    sx = v * sign(rng, (8, 1, NT)) * np.where(rng.random((8, 16, NT)) < rng.choice(p, (8, 1, NT)), -1, 1)
    sz[..., 0] = -v[None, :, :, 0]; sz[..., M - 1] = v[None, :, :, 0]; sx[..., 0] = -v[..., 0]; sx[..., NT - 1] = v[..., 0]
    d["z"] = np.where(sz > 0, 256, 8); d["x0"] = np.where(sx > 0, 256, 8)
    d["n0"] = atends(rng, d["n0"], M - 1, 0.8); d["n0"][:, 0] = 0; d["n0"][:, NT - 1] = M - 1
    d["nx"] = atends(rng, d["nx"], M - 1, 0.8); d["nx"][:, :, 0, 0] = 0; d["nx"][:, :, 2, M - 1] = M - 1
    d["nx"][:, 2, :, M - 1] = M - 1; d["nx"][:, 7, :, M - 1] = M - 1
    for g in range(8):
        d["hy"][:, g] = np.where(rng.random((N, KR, H)) < 0.78, (NT - 1) * rng.integers(0, 2, (N, KR, H)), rng.permutation(NT)[:60][rng.integers(0, 60, (N, KR, H))])
    d["u"] = atends(rng, rng.integers(0, 64, d["u"].shape), 63, 0.7)
    d["u"][:, 3] = 0; d["u"][:, 0] = 0; d["u"][N - 1, 0, :, KR - 1, H - 1] = 63; d["hy"][N - 1, 0, KR - 1, H - 1] = NT - 1
    quad(rng, d, 6, 3); hy, oc = deal(rng, NT); d["hy"][:, 6] = hy; d["u"][:, 6, 0] = np.array([0, 16, 32, 63])[oc % 4]
    return pack(d)
def setup_inputs_corners(rng):
    d = plain(rng); r = int(rng.integers(0, 8)); gs = [(r + i) % 8 for i in range(8)]
    for i in (0, 2, 4, 6): d["u"][:, gs[i]] = rng.integers(0, 64, (N, FR, KR, H))
    for i, s, one in ((1, NT, 0), (3, NT, 1), (5, NT - 1, 1)):
        g = gs[i]; quad(rng, d, g, 1); d["hy"][:, g] = deal(rng, s)[0]; d["u"][:, g] = 0
        if one: d["u"][N - 1, g, 0, KR - 1, H - 1] = 63
    g = gs[4]; quad(rng, d, g, 3); hy, oc = deal(rng, NT); d["hy"][:, g] = hy; d["u"][:, g, 0] = np.array([0, 16, 32, 63])[oc % 4]
    g = gs[6]; quad(rng, d, g, 1); hy, oc = deal(rng, NT // 2); d["hy"][:, g] = hy; d["u"][:, g, 0] = 63 * (oc % 2)
    d["z"][:, gs[7]] = far(rng, (FR, 16, M)); d["x0"][gs[7]] = np.minimum(d["x0"][gs[7]], 208)
    return pack(d)
def setup_inputs_crowd(rng):
    d = plain(rng); r = int(rng.integers(0, 8)); gs = [(r + i) % 8 for i in range(8)]
    for i in range(6): quad(rng, d, gs[i], 3)
    for i in range(7): d["u"][:, gs[i]] = rng.integers(0, 64, (N, FR, KR, H))
    a = rng.permutation(NT)
    d["hy"][:, gs[0]] = a[0]; d["u"][:, gs[0]] = 0
    d["hy"][:, gs[1]] = a[1]; d["hy"][N - 1, gs[1], KR - 1, H - 1] = a[2]; d["u"][:, gs[1], 0] = 0
    d["hy"][:, gs[2]] = NT - 1; d["u"][:, gs[2], 0] = 63
    d["hy"][:, gs[3]] = 0
    d["hy"][:, gs[4]] = (NT - 1) * rng.integers(0, 2, (N, KR, H))
    d["u"][:, gs[5], 0] = 0
    for q in range(N):
        f = rng.permutation(KR * H); d["hy"][q, gs[5]] = np.where(f < 256, a[3], np.where(f < 511, a[4], a[5])).reshape(KR, H)
    d["hy"][:, gs[6]] = a[6:9][rng.integers(0, 3, (N, KR, H))]
    return pack(d)
def setup_inputs_calm(rng):
    d = plain(rng); par = int(rng.integers(0, 2)); off = int(rng.integers(0, 4))
    for i in range(4):
        g = (2 * i + 1 + par) % 8; h = (g + 7) % 8; quad(rng, d, g, 1); d["hy"][:, g] = deal(rng, 64)[0]
        for t in range(FR):
            c = ((i + t + off) % 4) * 2 ** S + int(rng.integers(0, 2)) * (2 ** S - 1)
            d["u"][:, g, t] = np.where(rng.permutation(N * KR * H) < c, 0, 63).reshape(N, KR, H)
        d["u"][:, h] = np.where(rng.random((N, FR, KR, H)) < 0.5, rng.choice(np.array([8, 16, 24, 32]), (N, FR, KR, H)), rng.integers(0, 64, (N, FR, KR, H)))
    return pack(d)
def check_ranges(d):
    bad = []
    for k, lo, hi in (("nx", 0, M - 1), ("n0", 0, M - 1), ("hyp", 0, NT - 1), ("uu", 0, 63)):
        if np.min(d[k]) < lo or np.max(d[k]) > hi: bad.append("range of " + k)
    for k in ("z", "x0"):
        v = np.asarray(d[k], np.float64) * 32
        if not np.all((v >= 8) & (v <= 256) & (v == np.rint(v))): bad.append("range of " + k)
    for k in ("x0", "n0"):
        if np.any(np.asarray(d[k]) != np.asarray(d[k])[:1]): bad.append(k + " isn't alike on all ranks")
    return bad
def reference(z, nx, x0, n0, hyp, uu):
    zz = z.astype(np.float64).reshape(FR, PR, 8, 16, MS).transpose(0, 2, 3, 1, 4).reshape(FR, 8, 16, M)
    sx = nx.astype(np.int64).reshape(FR, PR, 8, 3, MS).transpose(0, 2, 3, 1, 4).reshape(FR, 8, 3, M)
    x = x0[0].astype(np.float64).reshape(8, 16, NT); n = n0[0].astype(np.int64)
    tr = np.stack([gentries(a) for a in hyp]).astype(np.int64).reshape(N, 8, KR, H)
    u = np.stack([gentries(a) for a in uu]).astype(np.int64).reshape(N, 8, FR, KR, H)
    live = np.ones((N, 8, KR, H), bool); w0 = np.full(8, 2, np.int64); gi = np.arange(8)[None, :, None]
    ye = np.zeros((N, 8, 16, H)); yx = np.zeros((N, 8, 16, H))
    for t in range(FR):
        nm = np.take_along_axis(sx[t], n[:, None, :], 2)
        zc = np.take_along_axis(zz[t], nm.reshape(8, 1, 3 * NT), 2).reshape(8, 16, 3, NT)
        dist = np.abs(zc - x[:, :, None, :])
        wt = np.maximum(np.add.reduce((dist <= 1).astype(np.int64), axis=1) - 4, 0)
        m = np.zeros((N, 8, KR, H), np.int64); took = np.full((N, 8, KR, H), -1, np.int64)
        for k in range(KR):
            T = tr[:, :, k]
            c = np.stack([nm[gi, i, T] for i in range(3)], axis=2); w = np.stack([wt[gi, i, T] for i in range(3)], axis=2)
            for j in range(k): w = np.where(c == took[:, :, j][:, :, None, :], 0, w)
            p = np.add.accumulate(np.concatenate([np.broadcast_to(w0[None, :, None, None], (N, 8, 1, H)), w], axis=2), axis=2)
            pick = np.argmax(64 * p > u[:, :, t, k][:, :, None, :] * p[:, :, 3:], axis=2)
            m[:, :, k] = pick
            name = np.take_along_axis(c, np.maximum(pick - 1, 0)[:, :, None, :], 2)[:, :, 0]
            took[:, :, k] = np.where(live[:, :, k] & (pick > 0), name, -1)
        pair = 4 * tr + m
        ex = np.exp(-np.concatenate([np.ones((8, 16, 1, NT)), dist], axis=2)).transpose(0, 1, 3, 2).reshape(8, 16, 4 * NT)
        for q in range(N):
            v = np.take_along_axis(ex, pair[q].reshape(8, 1, KR * H), 2).reshape(8, 16, KR, H)
            ye[q] = ye[q] + np.add.reduce(np.where(live[q][:, None], v, 0.0), axis=2)
        miss = np.add.reduce((live & (m == 0)).astype(np.int64), axis=(0, 2, 3))
        w0 = 1 + (np.roll(miss, -1) >> S)
        mark = np.zeros((8, 4 * NT), np.int64)
        for g in range(8): mark[g, pair[:, g][live[:, g]]] = 1
        place = np.add.accumulate(mark, axis=1) - mark
        xn = np.zeros((8, 16, NT)); nn = np.zeros((8, NT), np.int64)
        for g in range(8):
            o = np.nonzero(mark[g])[0][:NT]; T = o >> 2; hit = (o & 3) > 0; i = np.maximum((o & 3) - 1, 0); xo = x[g][:, T]
            xn[g][:, :len(o)] = np.where(hit, xo + 0.25 * (zc[g][:, i, T] - xo), xo)
            nn[g, :len(o)] = np.where(hit, nm[g, i, T], n[g, T])
        new = place[np.arange(8)[None, :, None, None], pair]
        live = live & (new < NT); tr = np.where(live, new, 0); x = xn; n = nn
    for q in range(N):
        v = np.take_along_axis(x, tr[q].reshape(8, 1, KR * H), 2).reshape(8, 16, KR, H)
        yx[q] = np.add.reduce(np.where(live[q][:, None], v, 0.0), axis=2)
    return {"ye": ye.reshape(N, 128, H).astype(np.float32), "yx": yx.reshape(N, 128, H).astype(np.float32)}

def check_inputs(d):
    bad = list(check_ranges(d))
    if not bad:
        for name, y in reference(**d).items():
            for q in range(N):
                v = np.abs(np.asarray(y[q], np.float64)); s = np.sqrt(np.mean(v * v))
                if v.max() > 7 * s or s < 2.0 ** -1: bad.append('%s of rank %d is uneven or too small' % (name, q))
    return bad

@@ -1,0 +1,712 @@
+from concourse.bass import DstId, RemoteDMATransfer
+from concourse.mybir import AluOpType as ALU, AxisListType, ActivationFunctionType as ACT
+
+F, B, I, U = "float32", "bfloat16", "int32", "uint16"
+SB = {
+    "zl": (1152, B), "Z0": (5120, B), "Z1": (4112, B), "nxw": (2048, I), "hu": (192, I),
+    "nt": (16, I), "nf": (16, F), "pint": (8, I), "pc": (24, B), "pf": (16, F), "colf": (128, B), "colq": (128, B),
+    "tmpd": (256, B), "cod": (64, B), "REP": (1024, B), "PERM": (128, B),
+    "RQ": (1024, B), "TRI": (128, B), "ONE": (1024, B), "ONF": (128, F), "IQ": (512, B), "iob": (128, B), "LW": (384, B),
+    "LN": (128, F), "LE": (1024, B), "CR": (768, B), "RW": (96, B), "R8": (8, B), "SEL": (24, F), "RN8": (16, F), "MB": (8, F),
+    "MN": (256, B), "LL": (256, F), "offc": (80, U), "offf": (80, F), "mrow": (512, B), "WL": (32, B), "ulut": (64, F),
+    "elut": (48, F), "RM": (64, F), "ni": (64, I), "nb": (128, I), "ucb": (128, U), "uc0": (32, U), "uz": (24, U), "uz1": (96, U),
+    "G0": (256, F), "mk1": (1024, F), "G1": (1024, F), "xg": (384, F), "xn": (512, F), "t96": (96, F),
+    "d0g": (384, F), "dq": (384, F), "ab": (1536, B), "near": (1536, B), "d1g": (1536, F), "tm": (512, B), "tb": (512, B),
+    "tab0": (1024, B), "tab1": (4096, B), "fe": (1024, B), "ue": (1024, B), "uh": (128, U), "tf": (384, F), "ti": (256, I),
+    "tfb": (64, B), "A": (8192, B), "Bm": (8192, B), "V": (512, F), "N": (512, F), "D": (512, F), "ub": (128, F), "R": (512, F),
+    "tt": (256, F), "cb": (528, F), "TK": (512, F), "ne": (192, F), "PAT": (768, F), "O0": (512, F), "O1": (256, B),
+    "uo1": (128, U), "mE": (1024, B), "mk": (128, F), "inc": (128, B), "cmp": (128, B), "th": (8, F), "sm": (640, F),
+    "ecol": (4, F), "ein": (4, F), "uo0": (64, U), "ut1": (64, U), "xr": (1024, B), "zr": (1024, B), "x1q": (1024, F),
+    "xw": (2056, F), "d1": (1024, F), "ad": (1024, F), "ex0": (1024, F), "uf": (96, U), "ye_s": (256, F), "yx_s": (256, F),
+}
+SCRATCH = {k: ("sbuf", [128, n], t) for k, (n, t) in SB.items()}
+SCRATCH.update({"P%d" % i: ("psum", [128, 512], F) for i in range(8)})
+SCRATCH.update({
+    "sz": ("dram", [8, 128, 128], B), "si": ("dram", [8, 128, 32], I), "li": ("dram", [8, 128, 32], I),
+    "sh": ("dram", [8, 128, 16], I), "lh": ("dram", [8, 128, 16], I), "rh": ("dram", [128, 16], I),
+    "rz": ("dram", [128, 128], B), "ri": ("dram", [128, 32], I), "rw": ("dram", [128, 1], F),
+    "lz": ("dram", [4, 128, 128], B), "dz": ("dram", [16, 4096], B),
+    "dt": ("dram", [16, 4096], B), "se": ("dram", [8, 128, 32], F), "sx": ("dram", [8, 128, 32], F),
+    "le": ("dram", [8, 128, 32], F), "lx": ("dram", [8, 128, 32], F), "re_": ("dram", [128, 32], F), "rx": ("dram", [128, 32], F),
+})
+SEMAPHORES = (["sv", "sa", "sp", "sg", "loc", "ain", "win", "oe", "ox", "ah", "r1", "r2", "r3", "r4", "r5", "r6"] + ["az%d" % i for i in range(8)]
+              + ["d%d" % i for i in range(25)])
+
+
+AHEAD = {"^vxw5": 5, "^aZ00": 6.4, "^vZ00": 5, "^gex04": 6, "^vye_s6": 1, "vsm6": -2.3, "^vth6": 5.3, "vxw5": -7.5, "vV5": 3,
+         "^ssx6": 1.5, "^vPAT4": 6, "vecol3": 3.7, "vtf6": 0.8, "vuf6": -7.5, "^aN4": 6, "^pP31": -6, "pP20": -6, "^vTK5": 0.7,
+         "^pP41": -1.5, "^vRW0": 3, "^vR5": 0.8, "vd16": 1.5, "^vO15": 0.7, "^pP70": 3, "^aue1": 3, "^vne3": -0.7, "^vO03": 3.0,
+         "^vCR0": 1.5, "^pP13": 0.7, "pP00": 1.5, "^pP01": 1.5, "vpc0": -6, "vO15": -0.7, "vni1": 6, "^gRQ0": -6, "vtmpd0": -6,
+         "pP01": -6, "^vuc00": -5.3, "vnf0": -3, "^pP34": -1.5, "^pP44": 0.7, "vtm1": -3, "vTK3": 6, "pP14": 6}
+
+
+AHEAD.update({"vxw5": 0, "pP20": -6.7, "vd16": -4.5, "^vO15": 0, "vpc0": 0, "vO15": 0, "vtmpd0": 0, "vnf0": 0, "^aue5": 3, "pP60": 6,
+              "^atm2": -0.7, "vTK5": -3, "aue1": -3, "^vMN0": -3, "^vuf6": 0.7, "vCR0": 3, "^sdz0": -3, "vth6": -3, "^velut0": -6,
+              "^vLE0": -0.7, "^vcmp6": -6, "vne5": 1.5, "^vpf0": 6, "^aD1": 0.7, "^vtt5": 0.7})
+
+
+def plan(T, topo, q):
+    me = T.cores[q]
+    dsts = [(q + i) % 8 for i in range(1, 8)]
+    direct = [d for d in dsts if topo.may_write(me, T.cores[d])]
+    eo = topo.engines(me, T.cores[direct[0]])
+    zdir = direct[:(len(eo) - len(direct)) // 2]
+    free = [c for c in topo.cores_of(me) if c != me]
+    rl = {}
+    for d in sorted([d for d in dsts if d not in zdir], key=lambda d: d in direct):
+        ok = [c for c in free if c not in rl.values() and topo.may_write(c, T.cores[d])]
+        rl[d] = min(ok, key=lambda c: (sum(topo.may_write(c, T.cores[e]) for e in dsts), topo.die(c) != topo.die(me)))
+    rest = [e for e in topo.engines(me, free[0]) if e not in eo]
+    return direct, zdir, rl, eo, rest
+
+
+def emask(es):
+    return sum(1 << e for e in es)
+
+
+def xfer(topo, src, dst, es, sem, a, b):
+    rid, pid = topo.addr(dst, src)
+    return RemoteDMATransfer(dst_ids=[DstId(rid=rid, pnc=pid)], dma_engine_mask=emask(es), remote_sem=sem, src=a, dst=b)
+
+
+def relay_program(g, core, T, topo, q, d, cross):
+    dc = T.cores[d]
+    es = topo.engines(core, dc)
+    h = len(es) // 2
+    S = T.sem
+    rid, pid = topo.addr(dc, core)
+    zl = T.zl[:, 128 * q:128 * q + 128] if q < 4 else T.lz[q - 4]
+    if not cross:
+        g.wait_ge(S.r1, 1)
+        g.remote_dma(zl, T.rz[:], S["az%d" % q], S.loc, pid, rid, emask(es))
+        g.wait_ge(S.loc, len(es))
+        return
+    g.wait_ge(S.r5, 1)
+    g.remote_dma(T.lh[q], T.rh[:], S.ah, S.loc, pid, rid, emask(es[:h // 2]))
+    g.wait_ge(S.r6, 1)
+    g.remote_dma(T.li[q], T.ri[:], S.ain, S.loc, pid, rid, emask(es[h // 2:h]))
+    g.wait_ge(S.r1, 1)
+    g.remote_dma(zl, T.rz[:], S["az%d" % q], S.loc, pid, rid, emask(es[h:]))
+    n = 3 * len(es)
+    if d == (q - 1) % 8:
+        g.wait_ge(S.r2, len(topo.engines(T.cores[q], core)))
+        g.remote_dma(T.ein[:, 0:1], T.rw[:], S.win, S.loc, pid, rid, emask(es))
+        n += len(es)
+    g.wait_ge(S.r3, 2)
+    g.remote_dma(T.le[q], T.re_[:], S.oe, S.loc, pid, rid, emask(es))
+    g.wait_ge(S.r4, 2)
+    g.remote_dma(T.lx[q], T.rx[:], S.ox, S.loc, pid, rid, emask(es))
+    g.wait_ge(S.loc, n)
+
+
+def rank_program(g, core, T, topo):
+    rank = T.rank_of(core)
+    if rank is None:
+        for q in range(len(T.cores)):
+            if core in topo.cores_of(T.cores[q]):
+                direct, zdir, rl, eo, rest = plan(T, topo, q)
+                for d, c in rl.items():
+                    if c == core:
+                        relay_program(g, core, T, topo, q, d, d not in direct)
+        return
+    me = rank
+    S = T.sem
+    plans = [plan(T, topo, q) for q in range(8)]
+    direct, zdir, rl, eo, rest = plans[me]
+    Q = {"v": g.vector, "a": g.scalar, "p": g.tensor, "g": g, "s": g.sync}
+    ops = []
+    recs = {}
+    group = {}
+    part = [0]
+    CY = 0.00104
+
+    def r(name, a=None, b=None, st=1, p=None):
+        t = T[name]
+        if a is None:
+            a, b = 0, t.shape[-1]
+        ps = slice(0, 128) if p is None else slice(p[0], p[1])
+        two = name in SB and SB[name][1] in (B, U)
+        return (t[ps, a:b:st] if st != 1 else t[ps, a:b], [(name, a, b)], (b - a + st - 1) // st, two, name not in SB, False)
+
+    def ind(w, o):
+        return (w[0].indirect(o[0]), w[1] + o[1], 16 * o[2], False, False, True)
+
+    def whole(name, ap=None):
+        return (T[name][:] if ap is None else ap, [(name, 0, 1 << 30)])
+
+    def regs(xs):
+        return [y for x in xs if isinstance(x, tuple) for y in x[1]]
+
+    def ap(x):
+        return x[0] if isinstance(x, tuple) else x
+
+    def add(e, fn, sem, inc, busy, lat, outs, ins, after=()):
+        me_ = len(ops)
+        pre = {x: False for x in after}
+        dm = sem[0] != "s"
+        for rs, wr in ((regs(ins), False), (regs(outs), True)):
+            for (n, a, b) in rs:
+                ps = n[0] == "P" and n[1:].isdigit()
+                for (a2, b2, o2, w2) in recs.get(n, []):
+                    e2, s2 = ops[o2][0], ops[o2][2]
+                    if dm and s2 == sem:
+                        continue
+                    if ps and e == "p" and e2 == "p":
+                        pre.setdefault(o2, False)
+                    elif (ps and e2 != e) or (a < b2 and a2 < b and (wr or w2)):
+                        for o3 in group.get(s2, [o2]):
+                            pre[o3] = True
+        for rs, wr in ((regs(ins), False), (regs(outs), True)):
+            for (n, a, b) in rs:
+                l = recs.setdefault(n, [])
+                if wr:
+                    l[:] = [x for x in l if not (a <= x[0] and x[1] <= b and pre.get(x[2]))]
+                l.append((a, b, me_, wr))
+        if dm:
+            group.setdefault(sem, []).append(me_)
+        ops.append([e, fn, sem, inc, busy, lat, pre, e + "".join(x[0] for x in regs(outs)[:1]) + str(part[0])])
+        return me_
+
+    def op(e, fn, out, ins, cost):
+        return add(e, fn, "s" + e, 1, cost, cost + 0.06, [out], ins)
+
+    def dma(e, sem, out, src, lat=2.3, after=(), **k):
+        return add(e, lambda: Q[e].dma_start(ap(out), ap(src), **k), sem, 16, 1.0 if e == "g" else 0.1, lat, [out], [src], after)
+
+    def arrive(sem, n, out, t, after=()):
+        return add("x", None, sem, n, 0.0, t, [out], [], after)
+
+    def remote(fn, n, ins, after=()):
+        return add("g", fn, "loc", -n, 0.6, 0.6, [], ins, after)
+
+    def landed(name, ap_):
+        return (ap_, [(name, 0, 1 << 31)])
+
+    def vcost(out, ins, two=False):
+        if ins[0][5]:
+            return 0.05 + out[2] * 1.56 * CY
+        f = 0.5 if all(x[3] for x in ins + [out] if isinstance(x, tuple)) else 1.0
+        if two:
+            f = 1.0 if ins[0][4] or ins[1][4] else 2.0
+        return max(64, max(out[2], ins[0][2]) * f) * CY
+
+    def ts(out, a, s1, o1, s2=None, o2=None):
+        if o2 is None:
+            op("v", lambda: g.vector.tensor_scalar(ap(out), ap(a), ap(s1), None, o1), out, [a, s1], vcost(out, [a, s1]))
+        else:
+            op("v", lambda: g.vector.tensor_scalar(ap(out), ap(a), ap(s1), ap(s2), o1, o2), out, [a, s1, s2], vcost(out, [a, s1, s2]))
+
+    def tt(out, a, b, o):
+        op("v", lambda: g.vector.tensor_tensor(ap(out), ap(a), ap(b), o), out, [a, b], vcost(out, [a, b], True))
+
+    def cp(out, a):
+        op("v", lambda: g.vector.tensor_copy(ap(out), ap(a)), out, [a], vcost(out, [a]))
+
+    def ms(out, c):
+        op("v", lambda: g.vector.memset(ap(out), c), out, [], vcost(out, [out]))
+
+    def scan(out, a, b):
+        op("v", lambda: g.vector.tensor_tensor_scan(ap(out), ap(a), ap(b), 0.0, ALU.mult, ALU.add), out, [a, b], vcost(out, [a, b]))
+
+    def red(out, a):
+        op("v", lambda: g.vector.tensor_reduce(ap(out), ap(a), AxisListType.X, ALU.add), out, [a], max(64, a[2]) * CY)
+
+    def act(out, a, f=ACT.Identity, scale=1.0, bias=0.0):
+        op("a", lambda: g.scalar.activation(ap(out), ap(a), f, bias=ap(bias), scale=ap(scale)), out, [a, scale, bias],
+           0.065 + out[2] * 1.56 * CY if a[5] else max(64, out[2]) * CY)
+
+    def mm(out, l, x, st=True, sp=True):
+        op("p", lambda: g.tensor.matmul(ap(out), ap(l), ap(x), st, sp), out, [l, x], max(64, x[2]) * (1 if x[3] else 4) * CY)
+
+    def iota(out, pat, base=0, cm=0, fl=True):
+        if fl:
+            op("g", lambda: g.iota(ap(out), pat, base, cm, allow_small_or_imprecise_dtypes=True), out, [], 0.13 + 2 * out[2] * CY)
+        else:
+            op("g", lambda: g.iota(ap(out), pat, base, cm), out, [], 0.13 + 2 * out[2] * CY)
+
+    def sel(out, a, pat, cmp_, base, cm):
+        op("g", lambda: g.affine_select(ap(out), ap(a), pat, cmp_, 0.0, base, cm), out, [a], 0.17 + 2 * out[2] * CY)
+
+    EQ, GE, LE_, LT, GT, NE = ALU.is_equal, ALU.is_ge, ALU.is_le, ALU.is_lt, ALU.is_gt, ALU.not_equal
+    ADD, SUB, MUL, MAX = ALU.add, ALU.subtract, ALU.mult, ALU.max
+    AND, SHR = ALU.bitwise_and, ALU.arith_shift_right
+    g0, g1 = 16 * me, 16 * me + 16
+
+    dma("s", "d0", whole("sh", T.sh[:, 0:64, :]), T.hyp[:])
+    dma("a", "d0", whole("sh", T.sh[:, 64:128, :]), T.uu[:, 0:64])
+    dma("s", "d11", whole("si", T.si[:, 0:96, :]), T.nx[:], 2.6)
+    dma("a", "d11", whole("si", T.si[:, 96:128, :]), T.uu[:, 64:128], 2.6)
+    dma("s", "d12", whole("sz"), T.z[:], 3.0)
+    dma("s", "d1", r("nt", p=(0, 64)), T.n0[me, :])
+    dma("a", "d2", r("mk"), T.x0[g0:g1, :])
+    if me < 4:
+        dma("a", "d4", r("zl", 128 * me, 128 * me + 128), T.z[g0:g1, :])
+    dma("s", "d3", whole("li", T.li[me, 0:96, :]), T.nx[3 * me:3 * me + 3, :])
+    dma("a", "d3", whole("li", T.li[me, 96:128, :]), T.uu[g0:g1, 64:128])
+    dma("s", "d13", whole("lh", T.lh[me, 0:64, :]), T.hyp[g0:g1, :])
+    dma("a", "d13", whole("lh", T.lh[me, 64:128, :]), T.uu[g0:g1, 0:64])
+    spare = eo[len(direct) + 2 * len(zdir):] + rest
+    cross = [d for d in rl if d not in direct]
+    sent = None
+    sends = []
+    for st, ld, rb, sd, sr in (("sh", "lh", "rh", "ah", "r5"), ("si", "li", "ri", "ain", "r6")):
+        tr = [xfer(topo, core, T.cores[d], [eo[i]], S[sd], T[st][d], T[ld][me]) for i, d in enumerate(direct)]
+        tr += [xfer(topo, core, rl[d], [spare[i]], S[sr], T[st][d], T[rb][:]) for i, d in enumerate(cross)]
+        sent = remote(lambda tr=tr: g.remote_dma_fused(tr, local_sem=S.loc), len(tr), [whole(st)], sends[-1:])
+        sends.append(sent)
+    ops[sends[0]][4] = 2.0
+    tz = [xfer(topo, core, rl[d], [spare[len(cross) + i]], S.r1, T.sz[d], T.rz[:]) for i, d in enumerate(rl)]
+    for i, d in enumerate(zdir):
+        j = len(direct) + 2 * i
+        tz.append(xfer(topo, core, T.cores[d], eo[j:j + 2], S["az%d" % me], T.sz[d],
+                       T.zl[:, 128 * me:128 * me + 128] if me < 4 else T.lz[me - 4]))
+    sent = remote(lambda: g.remote_dma_fused(tz, local_sem=S.loc), len(tz) + len(zdir), [whole("sz")], [sent])
+    ain, nout, late = 0, 0, {me: 0}
+    for q in range(8):
+        if q != me:
+            dq_, zq, rq = plans[q][:3]
+            n = len(topo.engines(rq[me], core)) if me in rq else 0
+            late[q] = 1 if me in zq else 2
+            arrive("az%d" % q, 2 if me in zq else n if me in dq_ else n // 2,
+                   r("zl", 128 * q, 128 * q + 128) if q < 4 else (None, [("lz", q, q + 1)]),
+                   4.2 if me in zq else 5.6, [sent])
+            ain += 1 if me in dq_ else n // 4
+            nout += 2 if me in dq_ else n
+    arrive("ain", ain, (None, [("li", 1 << 30, 1 << 31)]), 5.0, sends[1:])
+    arrive("ah", ain, (None, [("lh", 1 << 30, 1 << 31)]), 6.0, sends[:1])
+
+    iota(r("pint", 0, 1), [[0, 1]], 0, 1, False)
+    iota(r("iob"), [[1, 128]])
+    iota(r("colf"), [[0, 8], [1, 16]])
+    iota(r("colq"), [[1, 8], [0, 16]])
+    iota(r("cod", 0, 32), [[16, 8], [1, 4]])
+    iota(r("cod", 32, 56), [[1, 3], [4, 8]])
+    iota(r("offf", 0, 4), [[4, 4]])
+    iota(r("offf", 4, 16), [[0, 3], [16, 4]], 3)
+    iota(r("offf", 16, 22), [[8, 3], [48, 2]])
+    iota(r("sm", 0, 64), [[16, 64]], 8)
+    iota(r("mrow"), [[1, 4], [0, 128]])
+    iota(r("tt"), [[0, 256]], 1000000)
+    iota(r("PAT", 0, 256), [[0, 256]], 128)
+    iota(r("PAT", 256, 768), [[0, 512]], 1)
+    iota(r("WL"), [[1, 16], [0, 2]])
+    iota(r("elut"), [[1, 6], [1, 8]])
+    iota(r("t96", 0, 48), [[1, 6], [0, 8]])
+    iota(r("ONF"), [[0, 128]], 1)
+
+    for j, (s, o) in enumerate(((3, SHR), (7, AND), (4, SHR), (15, AND), (3, AND), (12, AND), (8, AND))):
+        ts(r("pint", j + 1, j + 2), r("pint", 0, 1), s, o)
+    cp(r("pc", 0, 8), r("pint"))
+    p_, p3, p7, p4, pf, pm, p12, p8 = [r("pc", j, j + 1) for j in range(8)]
+
+    def pcol(j):
+        return r("pc", j, j + 1)
+    ms(r("ONE"), 1.0)
+    sel(r("RQ"), r("ONE"), [[-16, 8], [0, 8], [-1, 16]], EQ, 0, 1)
+    sel(r("TRI"), r("ONE", 0, 128), [[1, 128]], GT, 0, -1)
+    sel(r("IQ", 0, 128), r("ONE", 0, 128), [[-1, 128]], EQ, 0, 1)
+    sel(r("R8"), r("ONE", 0, 8), [[-16, 8]], EQ, 0, 1)
+    for j, c in enumerate((-1.0, 0.25, 0.75)):
+        act(r("IQ", 128 * j + 128, 128 * j + 256), r("IQ", 0, 128), scale=c)
+    ms(r("nt", p=(64, 128)), 0)
+    ts(r("inc"), r("colf"), 8.0, MUL)
+    for ch in range(8):
+        ts(r("REP", 128 * ch, 128 * ch + 128), r("inc"), float(ch), ADD, p_, EQ)
+    cp(r("zl", 1024, 1152), r("mk"))
+    sel(r("PERM"), r("ONE", 0, 128), [[-1, 8], [-8, 16]], EQ, 0, 1)
+    ts(r("MN", 0, 128), r("colq"), p7, EQ)
+    ts(r("MN", 128, 256), r("colq"), p3, EQ)
+    ts(r("RN8", 0, 8), r("iob", 0, 8), p3, EQ)
+    ts(r("RN8", 8, 16), r("iob", 0, 8), p7, EQ)
+    ts(r("offc", 56, 64), r("iob", 0, 8), 0.0, MUL, pf, ADD)
+    cp(r("nf"), r("nt"))
+    for j in range(2):
+        tt(r("LL", 128 * j, 128 * j + 128), ind(r("nf"), r("offc", 56, 64)), r("MN", 128 * j, 128 * j + 128), MUL)
+        mm(r("P4", 8 * j, 8 * j + 8), r("LL", 128 * j, 128 * j + 128), r("RN8", 8 * j, 8 * j + 8))
+    for j in range(3):
+        mm(r("P5", 128 * j + 128, 128 * j + 256), r("PERM"), r("zl", 1024, 1152))
+    act(r("xg"), r("P5", 128, 512))
+    act(r("xn", 0, 128), r("P5", 128, 256))
+    cp(r("ni", 32, 40), r("P4", 0, 8))
+    cp(r("ni", 0, 8), r("P4", 8, 16))
+    for j, c in ((0, 32), (1, 0)):
+        ts(r("nb", 8 * j, 8 * j + 8), r("ni", c, c + 8), 1023, AND)
+        ts(r("nb", 16 + 8 * j, 24 + 8 * j), r("ni", c, c + 8), 10, SHR)
+    cp(r("uc0"), r("nb", 0, 32))
+    ts(r("MB"), r("iob", 0, 8), 4.0, MUL, p12, EQ)
+    act(r("mk1", 0, 256), ind(r("MB"), r("uc0", 16, 32)))
+    ts(pcol(8), p4, 4.0, MUL, pm, ADD)
+    ts(r("SEL"), r("cod", 32, 56), pcol(8), EQ)
+    ts(pcol(9), p4, 16.0, MUL)
+    for m in range(3):
+        ts(r("LW", 128 * m, 128 * m + 128), r("iob"), float(m - 2), ADD, pcol(9), EQ)
+    ts(pcol(10), pm, 3.0, EQ, 500.0, MUL)
+    ts(pcol(11), pm, -8.0, ADD, pcol(9), SUB)
+    ts(r("pf", 0, 1), pcol(11), pcol(10), ADD)
+    act(r("cmp"), r("iob"), ACT.Abs, 1.0, r("pf", 0, 1))
+    ts(r("LN"), r("cmp"), 2.0, EQ)
+    ts(r("pc", 21, 24), r("iob", 0, 3), pm, NE, 500.0, MUL)
+    ts(r("pc", 21, 24), r("pc", 21, 24), pcol(9), ADD)
+    ts(pcol(12), r("pf", 0, 1), -1.0, MUL)
+    for j in range(2):
+        for m in range(3):
+            ts(r("LE", 384 * j + 128 * m, 384 * j + 128 * m + 128), r("iob"), -12.0 - j, ADD, pcol(21 + m), EQ)
+        ts(r("LE", 768 + 128 * j, 896 + 128 * j), r("iob"), 2.0 - 4 * j, ADD, pcol(12), EQ)
+    ms(r("CR"), 0.0)
+    for c, v in ((11, 1.0), (14, 1.0), (128 + 14, 1.0), (256 + 7, 4096.0), (640 + 15, 1.0)):
+        ms(r("CR", c, c // 128 * 128 + 128, 16), v)
+    ts(r("CR", 384 + 12, 512, 16), r("iob", 0, 8), 128.0, MUL, 4096.0, ADD)
+    ts(r("CR", 512 + 7, 640, 16), r("iob", 0, 8), 128.0, MUL, 4096.0, ADD)
+    ts(r("CR", 512 + 12, 640, 16), r("iob", 0, 8), 512.0, MUL)
+    ts(pcol(15), pf, 7.5, GT, pf, MUL)
+    ts(pcol(14), pcol(15), 10.5, LT, p8, MUL)
+    ts(r("pf", 5, 6), pcol(14), 0.125, MUL)
+    lomask = r("pf", 5, 6)
+    for j, c in enumerate((0, 9, 10, 11, 4, 8, 5, 12)):
+        ts(r("tmpd", 32 * j, 32 * j + 32), r("cod", 0, 32), float(c), ADD, p_, EQ)
+    cp(r("RW", 0, 32), r("tmpd", 0, 32))
+    tt(r("RW", 3, 32, 4), r("tmpd", 35, 64, 4), r("tmpd", 67, 96, 4), ADD)
+    tt(r("RW", 3, 32, 4), r("RW", 3, 32, 4), r("tmpd", 99, 128, 4), ADD)
+    tt(r("RW", 32, 64), r("tmpd", 128, 160), r("tmpd", 160, 192), ADD)
+    tt(r("tmpd", 0, 32), r("tmpd", 192, 224), r("tmpd", 32, 64), ADD)
+    tt(r("RW", 64, 96), r("RW", 32, 64), r("tmpd", 0, 32), SUB)
+    cp(r("RW", 67, 96, 4), r("RW", 35, 64, 4))
+    tt(r("RW", 35, 64, 4), r("tmpd", 227, 256, 4), r("tmpd", 131, 160, 4), SUB)
+    act(r("ulut"), r("iob", 0, 64), ACT.Identity, -1.0 / 64, r("ONF", 0, 1))
+    ms(r("RM"), 1.0)
+    ms(r("RM", 0, 64, 4), 0.0)
+    ms(r("cb", 0, 528, 264), 0.0)
+    ms(r("Z1", 4096, 4112), 256.0)
+    ms(r("xw", 0, 8), 0.0)
+    ts(r("WL"), r("WL"), pf, EQ)
+    ts(r("WL", 1, 32, 2), r("WL", 1, 32, 2), 4096.0, MUL)
+    ts(pcol(17), pm, 3.0, NE)
+    ts(pcol(18), p12, 0.25, MUL)
+    ts(pcol(19), pm, 3.0, EQ, 16.0, MUL)
+    ts(r("offf", 0, 4), r("offf", 0, 4), pcol(18), ADD, pcol(17), MUL)
+    ts(r("offc", 0, 4), r("offf", 0, 4), pcol(19), ADD)
+    ts(r("offc", 4, 16), r("offf", 4, 16), p12, ADD)
+    ts(pcol(20), p8, 3.0, MUL, p7, ADD)
+    ts(r("offc", 16, 22), r("offf", 16, 22), pcol(20), ADD)
+    ts(r("sm", 0, 64), r("sm", 0, 64), pf, ADD)
+    act(r("th", 4, 5), r("ONF", 0, 1), ACT.Exp, -1.0)
+    ts(r("elut"), r("elut"), r("th", 4, 5), MUL)
+    tt(r("elut"), r("elut"), r("t96", 0, 48), SUB)
+
+    for t in range(2):
+        for a in range(8):
+            dma("sa"[a % 2] if t == 0 else "s", "d%d" % (5 + t), r("nxw", 1024 * t, 1024 * t + 1024, p=(16 * a, 16 * a + 16)),
+                landed("li", T.li[4 * t:4 * t + 4]), 3.0)
+    dma("s", "d7", r("hu", 0, 64), landed("lh", T.lh[:, 0:64, :]))
+    dma("a", "d8", r("hu", 64, 128), landed("lh", T.lh[:, 64:128, :]))
+    dma("s", "d22", r("hu", 128, 192), landed("li", T.li[:, 96:128, :]))
+    late[8] = 0
+    for q in range(4, 8):
+        dma("s", "d23", (T.dz[:, 1024 * q - 4096:1024 * q - 3072], [("dz", 0, 1)]),
+            T.z[g0:g1, :] if q == me else (T.lz[q - 4], [("lz", q, q + 1)]), 2.3, () if q == me else group["d6"])
+    for a in range(8):
+        dma("s", "d24", r("Z1", 0, 4096, p=(16 * a, 16 * a + 16)), whole("dz"), 4.4)
+    for i, q in enumerate(sorted([q for q in late if q // 4 != 1], key=lambda q: late[q])):
+        pa, pb = (("P0", "P1"), ("P2", "P3"), ("P6", "P7"))[i % 3]
+        for ch in range(8):
+            mm(r((pa, pb)[ch // 4], 128 * (ch % 4), 128 * (ch % 4) + 128), r("REP", 128 * ch, 128 * ch + 128),
+               r("zl", 128 * q, 128 * q + 128))
+        c = 1024 * (q if q < 4 else 4)
+        (cp if late[q] == 2 else act)(r("Z0", c, c + 512), r(pa))
+        act(r("Z0", c + 512, c + 1024), r(pb))
+
+    part[0] = 1
+    tt(r("G0"), ind(r("nxw", 0, 1024), r("uc0", 0, 16)), r("mk1", 0, 256), MUL)
+    mm(r("P4", 16, 40), r("G0", 0, 128), r("SEL"))
+    mm(r("P4", 40, 64), r("G0", 128, 256), r("SEL"))
+    cp(r("uh", 0, 64), r("hu", 0, 64))
+    cp(r("uh", 64, 128), r("hu", 64, 128))
+    ts(r("ti", 0, 64), r("hu", 0, 64), 3, SHR)
+    ts(r("ti", 64, 128), r("hu", 0, 64), 7, AND)
+    cp(r("tfb"), r("ti", 0, 64))
+    cp(r("uz"), r("P4", 16, 40))
+    cp(r("ni", 8, 32), r("P4", 16, 40))
+    cp(r("ni", 40, 64), r("P4", 40, 64))
+    tt(r("d0g"), ind(r("Z0", 0, 4096), r("uz")), r("xg"), SUB)
+    act(r("ab", 0, 384), r("d0g"), ACT.Abs)
+    act(r("dq"), r("d0g"), scale=0.25)
+    ts(r("nb", 0, 64), r("ni"), 1023, AND)
+    ts(r("nb", 64, 128), r("ni"), 10, SHR)
+    cp(r("ucb"), r("nb"))
+    ts(r("near", 0, 384), r("ab", 0, 384), 1.0, LE_)
+    act(r("tm", 0, 128), r("G0", 128, 256))
+    tt(r("tm", 128, 256), r("G0", 128, 256), r("tm", 0, 128), SUB)
+    for j in range(2):
+        mm(r("P4", 256, 384), r("LE", 768 + 128 * j, 896 + 128 * j), r("tm", 128 * j, 128 * j + 128), j == 0, False)
+    mm(r("P4", 256, 384), r("CR", 0, 128, p=(0, 1)), r("iob", p=(0, 1)), False, False)
+    mm(r("P4", 256, 384), r("CR", 512, 640, p=(0, 1)), r("ONE", 0, 128, p=(0, 1)), False, False)
+    for m in range(3):
+        mm(r("P4", 256, 384), r("LW", 128 * m, 128 * m + 128), r("near", 128 * m, 128 * m + 128), False, m == 2)
+    cp(r("tb", 0, 128), r("P4", 256, 384))
+    for q in range(8):
+        mm(r("P%d" % (q // 4), 128 * (q % 4), 128 * (q % 4) + 128), r("RQ", 128 * q, 128 * q + 128), r("tb", 0, 128))
+    cp(r("tab0", 0, 512), r("P0"))
+    act(r("tab0", 512, 1024), r("P1"))
+    for k in range(4):
+        act(r("fe", 256 * k, 256 * k + 256), ind(r("tab0"), r("uh", 16 * k, 16 * k + 16)))
+
+    def fields(h):
+        for u in range(4 * h, 4 * h + 4):
+            for w in range(3):
+                c = 128 * w + 32 * (u % 4)
+                mm(r("P%d" % (2 + h), c, c + 32), r("fe", 128 * u, 128 * u + 128), r("RW", 32 * w, 32 * w + 32))
+
+    def evac(t, h):
+        o = 256 * t + 128 * h
+        pb = "P%d" % (2 + h)
+        ts(r("V", o, o + 128), r(pb, 0, 128), -4.0, ADD, 0.0, MAX)
+        if t == 0:
+            cp(r("PAT", o + 3, o + 128, 4), r(pb, 3, 128, 4))
+            cp(r("ti", 128 + 32 * h, 160 + 32 * h), r(pb, 3, 128, 4))
+            ms(r("V", o + 3, o + 128, 4), 2.0)
+        else:
+            cp(r("uo0", 32 * h, 32 * h + 32), r(pb, 3, 128, 4))
+        act(r("D", o, o + 128), r(pb, 256, 384))
+        act(r("N", o, o + 128), r(pb, 128, 256))
+    for h in range(2):
+        fields(h)
+        evac(0, h)
+    ts(r("ti", 192, 256), r("ti", 128, 192), 7, AND)
+    ts(r("PAT", 259, 512, 4), r("ti", 192, 256), 4.0, MUL)
+    for h in range(2):
+        act(r("ue", 512 * h, 512 * h + 512), ind(r("ulut"), r("uh", 64 + 32 * h, 96 + 32 * h)))
+    for u in range(8):
+        mm(r("P5", 8 * u, 8 * u + 8), r("ue", 128 * u, 128 * u + 128), r("R8"))
+    act(r("ub", 0, 64), r("P5", 0, 64))
+    for c in range(64):
+        ts(r("A", 128 * c, 128 * c + 128), r("iob"), r("tfb", c, c + 1), EQ)
+
+    part[0] = 2
+    act(r("mk1", 512, 1024), ind(r("MB"), r("ucb", 96, 128)))
+    tt(r("G1", 512, 1024), ind(r("nxw", 1024, 2048), r("ucb", 32, 64)), r("mk1", 512, 1024), MUL)
+    for m in range(4):
+        mm(r("P6", 24 * m, 24 + 24 * m), r("G1", 512 + 128 * m, 640 + 128 * m), r("SEL"))
+    act(r("t96"), r("P6", 0, 96))
+    cp(r("uz1"), ind(r("t96"), r("offc", 16, 22)))
+    tt(r("xn", 128, 512), r("P5", 128, 512), r("dq"), ADD)
+    act(r("mk1", 0, 512), ind(r("MB"), r("ucb", 64, 96)))
+    tt(r("G1", 0, 512), ind(r("nxw", 1024, 2048), r("ucb", 0, 32)), r("mk1", 0, 512), MUL)
+    mm(r("P7"), r("CR", 256, 384, p=(0, 1)), r("ONE", 0, 512, p=(0, 1)), True, False)
+    mm(r("P7"), r("CR", 640, 768, p=(0, 1)), r("mrow", p=(0, 1)), False, False)
+    mm(r("P7", 0, 128), r("CR", 128, 256, p=(0, 1)), r("iob", p=(0, 1)), False, False)
+    mm(r("P7", 0, 128), r("CR", 384, 512, p=(0, 1)), r("ONE", 0, 128, p=(0, 1)), False, False)
+    for m in range(3):
+        for j in range(2):
+            mm(r("P7", 128 * m + 128, 128 * m + 256), r("LE", 384 * j + 128 * m, 384 * j + 128 * m + 128),
+               r("tm", 128 * j, 128 * j + 128), False, False)
+    for m in range(4):
+        mm(r("P7", 128 * m, 128 * m + 128), r("LN"), r("G1", 128 * m, 128 * m + 128), False, False)
+    for m in range(3):
+        a, b = 512 * m, 512 * m + 512
+        tt(r("d1g", a, b), ind(r("Z1", 0, 4096), r("uz1", 32 * m, 32 * m + 32)), r("xn"), SUB)
+        act(r("ab", a, b), r("d1g", a, b), ACT.Abs)
+        ts(r("near", a, b), r("ab", a, b), 1.0, LE_)
+        mm(r("P7"), r("LW", 128 * m, 128 * m + 128), r("near", a, b), False, m == 2)
+    act(r("tm"), r("P7"), scale=lomask)
+    tt(r("tb"), r("P7"), r("tm"), SUB)
+    for q in range(8):
+        dma("s", "d9", whole("dt", T.dt[:, 512 * q:512 * q + 512]), r("tb", p=(16 * q, 16 * q + 16)), 2.4)
+    for a in range(8):
+        dma("s", "d10", r("tab1", p=(16 * a, 16 * a + 16)), whole("dt"), 4.4)
+
+    def draw(t, k):
+        o = 256 * t + 64 * k
+        c = 264 * t + 64 * k
+        scan(r("R", o, o + 64), r("RM"), r("V", o, o + 64))
+        w = 128 * t + 32 * k
+        tt(r("tt", w, w + 16), r("R", o + 3, o + 64, 4), r("ub", 64 * t + 16 * k, 64 * t + 16 * k + 16), MUL)
+        tt(r("cb", c + 1, c + 65), ind(r("tt", w, w + 24), r("offc", 0, 4)), r("R", o, o + 64), LE_)
+        if t == 1 or k < 3:
+            scan(r("TK", o, o + 64), r("cb", c, c + 64), r("D", o, o + 64))
+        if k < 3:
+            n = 64 * (3 - k)
+            tt(r("ne", 0, n), ind(r("TK", o, o + 64), r("offc", 4, 4 + n // 16)), r("N", o + 64, o + 64 + n), NE)
+            tt(r("V", o + 64, o + 128), r("V", o + 64, o + 128), r("ne", 0, 64), MUL)
+            if k < 2:
+                tt(r("V", o + 128, o + 64 + n), r("V", o + 128, o + 64 + n), r("ne", 64, n), MUL)
+        return r("cb", c, c + 64)
+
+    part[0] = 3
+    for k in range(4):
+        c = draw(0, k)
+        scan(r("O0", 128 * k, 128 * k + 64), c, r("PAT", 64 * k, 64 * k + 64))
+        scan(r("O0", 128 * k + 64, 128 * k + 128), c, r("PAT", 256 + 64 * k, 320 + 64 * k))
+        cp(r("uo1", 32 * k, 32 * k + 32), r("O0", 128 * k + 3, 128 * k + 128, 4))
+        act(r("mE", 256 * k, 256 * k + 256), ind(r("WL"), r("uo1", 32 * k + 16, 32 * k + 32)))
+        pb = "P%d" % (k % 2)
+        for j in range(2):
+            mm(r(pb, 128 * j, 128 * j + 128), r("mE", 256 * k + 128 * j, 256 * k + 128 * j + 128), r("IQ", 0, 128))
+        act(r("Bm", 256 * k, 256 * k + 256), r(pb, 0, 256))
+        for c in range(16 * k, 16 * k + 16):
+            mm(r("P6", 16 * k, 16 * k + 16), r("A", 128 * c, 128 * c + 128), r("Bm", 16 * c, 16 * c + 16), c % 16 == 0, c % 16 == 15)
+    red(r("ecol", 0, 1), r("cb", 3, 256, 4))
+    d = (me - 1) % 8
+    to = T.cores[d] if d in direct else rl[d]
+    rid, pid = topo.addr(to, core)
+    ee = topo.engines(core, to)
+    if d in direct:
+        sent = remote(lambda: g.remote_dma(T.ein[:, 0:1], T.ecol[:, 0:1], S.win, S.loc, pid, rid, emask(ee)), len(ee), [r("ecol")])
+    else:
+        sent = remote(lambda: g.remote_dma(T.rw[:], T.ecol[:, 0:1], S.r2, S.loc, pid, rid, emask(ee)), len(ee), [r("ecol")])
+    part[0] = 4
+    q = (me + 1) % 8
+    arrive("win", len(topo.engines(T.cores[q] if me in plans[q][0] else plans[q][2][me], core)), r("ein"), 5.5, [sent])
+    for k in range(4):
+        act(r("fe", 256 * k, 256 * k + 256), ind(r("tab1"), r("uo1", 32 * k, 32 * k + 16)))
+    for h in range(2):
+        fields(h)
+        evac(1, h)
+        act(r("xr", 512 * h, 512 * h + 512), ind(r("Z0", 4096, 5120), r("uh", 32 * h, 32 * h + 32)))
+        act(r("zr", 512 * h, 512 * h + 512), ind(r("Z0"), r("uo0", 32 * h, 32 * h + 32)))
+    ts(r("tf", 128, 192), r("ti", 64, 128), 4.0, MUL, 4096.0, ADD)
+    tt(r("tf", 64, 128), r("tf", 128, 192), r("N", 259, 512, 4), ADD)
+    ts(r("tf", 192, 256), r("tfb"), 32.0, MUL)
+    tt(r("tf", 192, 256), r("tf", 192, 256), r("tf", 64, 128), ADD)
+    act(r("tf", 64, 128), r("tf", 64, 128), scale=4.0)
+    ts(r("ub", 64, 128), r("hu", 128, 192), -1.0 / 64, MUL, 1.0, ADD)
+    ts(r("sm", 128, 192), r("N", 259, 512, 4), -4096.0, EQ, 8.0, MUL)
+
+    def theta(src, n, t):
+        ts(r("mk", 0, n), src, 0.5, GT)
+        scan(r("inc", 0, n), r("ONE", 0, n), r("mk", 0, n))
+        mm(r("P7", 0, 1), r("TRI"), r("inc", n - 1, n))
+        ts(r("cmp", 0, n), r("inc", 0, n), r("P7", 0, 1), ADD, 1024.5, LT)
+        mm(r("P7", 128, 128 + n), r("ONE", 0, 128), r("cmp", 0, n))
+        red(r("th", t, t + 1), r("P7", 128, 128 + n))
+    cp(r("ni"), r("P6", 0, 64))
+    ts(r("nb", 0, 128, 2), r("ni"), 4095, AND)
+    ts(r("nb", 1, 128, 2), r("ni"), 12, SHR)
+    tt(r("sm", 512, 576), r("nb", 0, 64), r("nb", 64, 128), ADD)
+    tt(r("sm", 576, 608), r("sm", 512, 544), r("sm", 544, 576), ADD)
+    theta(r("sm", 576, 608), 32, 0)
+    mm(r("P4", 0, 1), r("ONF"), r("ein", 0, 1))
+    ts(r("ti", 0, 1), r("P4", 0, 1), -1.0, MUL, 9216.0, ADD)
+    ts(r("ti", 1, 2), r("ti", 0, 1), 10, SHR)
+    cp(r("th", 2, 3), r("ti", 1, 2))
+    ts(r("V", 259, 512, 4), r("V", 259, 512, 4), 0.0, MUL, r("th", 2, 3), ADD)
+    ts(r("sm", 192, 256), r("tf", 192, 256), r("th", 0, 1), GE)
+    tt(r("ub", 64, 128), r("ub", 64, 128), r("sm", 192, 256), MAX)
+    ts(r("sm", 256, 320), r("tf", 192, 256), r("th", 0, 1), GE, 100000.0, MUL)
+    tt(r("PAT", 515, 768, 4), r("sm", 256, 320), r("tf", 64, 128), ADD)
+
+    for h in range(2):
+        a, b = 512 * h, 512 * h + 512
+        mm(r("P%d" % h), r("IQ", 384, 512), r("xr", a, b), True, False)
+        mm(r("P%d" % h), r("IQ", 256, 384), r("zr", a, b), False, True)
+        act(r("xw", 8 + a, 8 + b), r("P%d" % h))
+    for h in range(2):
+        a, b = 512 * h, 512 * h + 512
+        mm(r("P%d" % (4 + h)), r("IQ", 128, 256), r("xr", a, b), True, False)
+        mm(r("P%d" % (4 + h)), r("IQ", 0, 128), r("zr", a, b), False, True)
+        act(r("G1", a, b), r("P%d" % (4 + h)), ACT.Abs)
+        act(r("ex0", a, b), r("G1", a, b), ACT.Exp, -1.0)
+    dma("g", "d14", r("ex0", 0, 512), r("ex0", 512, 1024), 3.5, accum_op=ADD)
+    dma("g", "d15", r("ex0", 0, 256), r("ex0", 256, 512), 3.0, accum_op=ADD)
+
+    part[0] = 5
+    for k in range(4):
+        c = draw(1, k)
+        scan(r("O1", 64 * k, 64 * k + 64), c, r("PAT", 512 + 64 * k, 576 + 64 * k))
+        cp(r("ut1", 16 * k, 16 * k + 16), r("TK", 256 + 64 * k + 3, 256 + 64 * k + 64, 4))
+        for c in range(16 * k, 16 * k + 16):
+            ts(r("Bm", 128 * c, 128 * c + 128), r("iob"), r("O1", 4 * c + 3, 4 * c + 4), EQ)
+            mm(r("P6", 0, 128), r("A", 128 * c, 128 * c + 128), r("Bm", 128 * c, 128 * c + 128), c == 0, c == 63)
+        a, b = 256 * k, 256 * k + 256
+        act(r("ue", a, b), ind(r("Z1"), r("ut1", 16 * k, 16 * k + 16)))
+        tt(r("d1", a, b), r("ue", a, b), r("P%d" % (k // 2), 256 * (k % 2), 256 * (k % 2) + 256), SUB)
+        act(r("x1q", a, b), r("d1", a, b), scale=0.25)
+        act(r("ad", a, b), r("d1", a, b), ACT.Abs)
+        act(r("P%d" % (2 + k), 0, 256), r("ad", a, b), ACT.Exp, -1.0)
+        tt(r("xw", 1032 + a, 1032 + b), r("P%d" % (k // 2), 256 * (k % 2), 256 * (k % 2) + 256), r("x1q", a, b), ADD)
+    part[0] = 6
+    hit = r("cb", 264 + 3, 264 + 256, 4)
+    act(r("tf", 256, 320), r("tfb"), scale=128.0)
+    tt(r("tf", 256, 320), r("tf", 256, 320), r("O1", 3, 256, 4), ADD)
+    act(r("tf", 320, 384), hit, scale=1024.0)
+    tt(r("tf", 320, 384), r("tf", 320, 384), r("sm", 0, 64), ADD)
+    tt(r("sm", 320, 384), hit, r("sm", 192, 256), MAX)
+    tt(r("sm", 320, 384), r("sm", 128, 192), r("sm", 320, 384), SUB)
+    tt(r("sm", 384, 416), r("sm", 320, 352), r("sm", 352, 384), ADD)
+    tt(r("sm", 416, 432), r("sm", 384, 400), r("sm", 400, 416), ADD)
+    ts(r("uf", 64, 80), r("sm", 416, 432), 4.0, ADD)
+    tt(r("ye_s"), ind(r("elut"), r("uf", 64, 80)), r("ex0", 0, 256), ADD)
+    for k in range(4):
+        tt(r("ye_s"), r("P%d" % (2 + k), 0, 256), r("ye_s"), ADD)
+    theta(r("P6", 0, 128), 128, 1)
+    ts(r("sm", 448, 512), r("tf", 256, 320), r("th", 1, 2), LT)
+    tt(r("sm", 448, 512), r("sm", 448, 512), r("tf", 320, 384), MUL)
+    cp(r("uf", 0, 64), r("sm", 448, 512))
+    act(r("d1", 0, 256), ind(r("xw"), r("uf", 0, 16)))
+    cp(r("d1", 256, 512), ind(r("xw"), r("uf", 16, 32)))
+    tt(r("d1", 512, 768), ind(r("xw"), r("uf", 32, 48)), r("d1", 256, 512), ADD)
+    tt(r("d1", 768, 1024), ind(r("xw"), r("uf", 48, 64)), r("d1", 0, 256), ADD)
+    tt(r("yx_s"), r("d1", 512, 768), r("d1", 768, 1024), ADD)
+
+    for i, (src, st, ld, rb, sr, so, out) in enumerate((("ye_s", "se", "le", "re_", "r3", "oe", T.ye),
+                                                        ("yx_s", "sx", "lx", "rx", "r4", "ox", T.yx))):
+        dma("s", "d%d" % (16 + 3 * i), whole(st), r(src))
+        dma("a", "d%d" % (17 + 3 * i), whole(ld, T[ld][me]), r(src, p=(g0, g1)))
+        tr_ = [xfer(topo, core, T.cores[d], eo[2 * j:2 * j + 2], S[so], T[st][d], T[ld][me]) for j, d in enumerate(direct)]
+        tr_ += [xfer(topo, core, rl[d], rest[2 * j:2 * j + 2], S[sr], T[st][d], T[rb][:])
+                for j, d in enumerate([d for d in rl if d not in direct])]
+        sent = remote(lambda tr_=tr_: g.remote_dma_fused(tr_, local_sem=S.loc), 2 * len(tr_), [whole(st)])
+        arrive(so, nout, (None, [(ld, 1, 2)]), 5.0, [sent])
+        dma("s", "d%d" % (18 + 3 * i), out[:], whole(ld))
+
+    n = len(ops)
+    succ = [[] for _ in range(n)]
+    for i, o in enumerate(ops):
+        for j in o[6]:
+            succ[j].append(i)
+    prio = [0.0] * n
+    for i in range(n - 1, -1, -1):
+        prio[i] = ops[i][5] + AHEAD.get("^" + ops[i][7], 0.0) + max([prio[j] for j in succ[i]] + [0.0])
+    prio = [x + AHEAD.get(o[7], 0.0) for x, o in zip(prio, ops)]
+    left = [len(o[6]) for o in ops]
+    ready = [0.0] * n
+    free = {e: 0.0 for e in list(Q) + ["x"]}
+    cand = {e: [] for e in free}
+    for i in range(n):
+        if not left[i]:
+            cand[ops[i][0]].append(i)
+    cnt = {}
+    val = [0] * n
+    known = {e: {} for e in Q}
+    for _ in range(n):
+        t0, e = min((max(free[e], min(ready[i] for i in c)), e) for e, c in cand.items() if c)
+        now = [i for i in cand[e] if ready[i] <= t0]
+        i = max(now, key=lambda i: prio[i])
+        soon = [j for j in cand[e] if t0 < ready[j] < t0 + 0.6 * ops[i][4] and prio[j] > prio[i] + 1.0]
+        if soon:
+            i = min(soon, key=lambda j: ready[j])
+        cand[e].remove(i)
+        e, fn, sem, inc, busy, lat, pre = ops[i][:7]
+        t0 = max(t0, ready[i])
+        free[e] = t0 + busy
+        for j in succ[i]:
+            ready[j] = max(ready[j], t0 + (lat if ops[j][6][i] or ops[j][0] == "x" else busy))
+            left[j] -= 1
+            if not left[j]:
+                cand[ops[j][0]].append(j)
+        if e != "x":
+            need = {}
+            for j, w in pre.items():
+                if w and ops[j][2] != "loc":
+                    need[ops[j][2]] = max(need.get(ops[j][2], 0), val[j])
+            for s2, v2 in need.items():
+                if known[e].get(s2, 0) < v2:
+                    Q[e].wait_ge(S[s2], v2)
+                    known[e][s2] = v2
+            call = fn()
+            if inc > 0:
+                call.then_inc(S[sem], inc)
+        cnt[sem] = cnt.get(sem, 0) + abs(inc)
+        val[i] = cnt[sem]
+    for s2, v2 in cnt.items():
+        if known["g"].get(s2, 0) < v2:
+            g.wait_ge(S[s2], v2)

@@ -25,7 +25,7 @@ SCRATCH.update({
     "sz": ("dram", [8, 128, 128], B), "si": ("dram", [8, 128, 32], I), "li": ("dram", [8, 128, 32], I),
     "sh": ("dram", [8, 128, 16], I), "lh": ("dram", [8, 128, 16], I), "rh": ("dram", [128, 16], I),
     "rz": ("dram", [128, 128], B), "ri": ("dram", [128, 32], I), "rw": ("dram", [128, 1], F),
-    "lz": ("dram", [4, 128, 128], B), "dz": ("dram", [16, 4096], B),
+    "lz": ("dram", [8, 128, 128], B), "dz": ("dram", [16, 4096], B),
     "dt": ("dram", [16, 4096], B), "se": ("dram", [8, 128, 32], F), "sx": ("dram", [8, 128, 32], F),
     "le": ("dram", [8, 128, 32], F), "lx": ("dram", [8, 128, 32], F), "re_": ("dram", [128, 32], F), "rx": ("dram", [128, 32], F),
 })
@@ -45,12 +45,20 @@ AHEAD.update({"vxw5": 0, "pP20": -6.7, "vd16": -4.5, "^vO15": 0, "vpc0": 0, "vO1
               "^vLE0": -0.7, "^vcmp6": -6, "vne5": 1.5, "^vpf0": 6, "^aD1": 0.7, "^vtt5": 0.7})
 
 
+ORDER = (
+    "03020605080c090a070o0m0v1u22252627282f2i2e231g000u0j0t2q013x413g643h5v494d3k5w4b3w0r0w0q0s0e0p0f0x045h5z4v3r5x6saz181314291o1s1k1p1m1w1c2u0z151b1i171e1f1j1h1n2v2x2y3m3o1r2b1v242h2c2j202l0y19103j4g5p1112161a4a2m371d3q3e774t7c4x5k1l2g2k2o42464o443t3u333d742s2r2w2t302z313b34383l3a353c3f3i4e3y4w2n48el3s3v365m405n7p432p45ft6e797g4s534h513z524c4u897q7a7e7n83877r3p3nam9k9n9m9l9za3a59ya0a1a4a20g0b0i0d0l0h0n0k5i5f6t586k5d68555j5c6n5666546a5969575y5e625b6j5a1y2a2d321q1t1x1z39215q60634k4i4f4l4jeg6l6m6o6u6y7h6x6w6z715t6b6p6q6r6v7576787j7k7l7m7x7o7z80818d828j8s9b9r8k8l8m8n8o8p8t8u8v8w8x9091929j9a9p9q9c9d9e9f9g9h9s9t9u9v9w9xagafahbdatasaqav5g5r6f6g6h6i72737b8485c34n5l7s67657u5obpccbe5scscgd086d5d84m6c7tc94y50ct88dwdme5due2do4z5ue8ds7ieh7ye6dbe0edebeteee3eaek7df3fieoejeueneserdvfue9e7frfs708a8b8c7w8g8h8i8y8z8r7v8q474p4q4r6d7f8e8f939495969899a6a8a9aba7acadaiaaajakanaeaoapawaxb4bcbob5bsb6brb7bgbwcybtcnbucrbvcz9i9oalarayb1bhaub0b2b8babbbyc4c5c6c7cacbcecfcjckcmcqcvcwd3d4b3b9bfbibkbmc0blbjbnbxbzc2cld6d9dadddedfdgdhdidxdye1efeqevewbqc1c8cdcicpchcocxd2dpdze4exeyezf0f1f2f4f5f6f8f9fafbfcfdfecud1d7dkdjdqdremepf7fffgfhfjfkflfmfnfofpfqfvfwfxfyfzdcdldng8g5gagig9gbgcgegfggghgkglgmgngogygpgqh8hm61grgsgtgugvgwgxgzh0h1h2h3h4hgh9h5hyhl97hieihahbecmmg0g1g2g3g4gdgjh6h7hehfhchdhjhohphnhzhki1ixiyjsg7ieiuhhhqhrhug6hshthvhwhxi0i2i3i4i6i8ici5j6ifj1ikklinkmilknijkoiskpiwkqirkriqksj4ktigkuj9kvi7kwipkxiaiikyi9ibkzjek5kdmsmvmaidihimioitj0jfivkejdl0jil1jgl2j3l3jjl4j2l5jml6jll7jrl8jql9k0lajblbjylcjzleizj8loj7jalukim6m8m9mgnij5jcjhjkjnjpjokgk7lvkalykbm3k9m5kjmfk2mhlgmlk4mnkkmplpmrlhmwlkmxldmyk6n0jwjxn1jujvn2khm0m1mcmjnljtk1k3k8lfkclzn6lrn7m4n8lqn9lmnbmbncmdndlxnemenfm7ngmunhmtnjmonkminnlilnnoljlwnpkflsltmkmqmzdtnam2n4lln3n5nmnsnwnyo0o4o6nqnrntnunvnxnzo1o2o3o5obocodo8o7o9oaogofoeohoioj")
+
+
+ORDER = (
+    "03020605080b090a070g0f1j1t202324254r2c2f2b211k000m0e0l2o013r3w3e693b5m4a4d3g5n3u3p0j0n0i0k0c0h0d0o044l624h3jad9nau0z0u0v261e1q1a1n1c1v131f0q0w12180y151619171d1g1h1i1l1m1p281u222e292g1z5b0p100r3d4c5p0s0t0x11472j31143i397i617j4i641b2d2h2l3y453l433m3n2x387c2q2p2s2r2u2t2v342y323h332z353a3c4e50562k46ee3k3o304q3s4v8y3z2n44ez6t7h7m5t4t5258575a5s4y807z7u68747e6j751s40ab799o919p9s9q9t9r9w9x9v9u48364u3f414b3x373v426k4f2i3t2m3q1x272a2w1o1r1w1y6h5e4m4n4o4z5f5g5h5i5o60595k5q5v4s545c5d5x5y5w63654p4j4g494kfw66676e6l6z776r6s6x706i6u6q6v6w6y7172767o7q7v7w7y7r7s7t818d828g8n989f8h8i8j8k8l8m8o8p8q8r8s8z9ka2aja1akal999a9b9c9d9e9g9h9i9j9l9maianambiasaravax6c5j6f6g6m6n6p787d7l86bx4x537xc0877n4wclc8bn8uc3cicy7gbpd7555184b25u5rdocgdvdde3dte4dn5le2ecdu7feg8te0elebeaedepe6eie9ej73ereueneheqefeoesdwfvete8exey7a888a8b7b898c8e8w8x8v7p8f5z6a6b6d6o7k83859293949596979ya3a6a8a0a5aaac9za4afaha9aeapaqatb8bgbfbbbdbcbabeb9bwd2btd9bucpbvd1a7agaoawayb1bkazb0b3b5b6b7byc4c5c6c7c9cacecfcqcrcvcwcxczd3d4b4bhbjblbobrccbmbqbsc1ckcncod5d8dbdcdedfdgdkdpdxdye1emewf0f1bzc2cbcdchcjctcsd0dadqdze5f2f3f6f7f8f9fafbfcfdfefffgfhfifjcmcud6dmdldrdsevf4f5fkflfmfnfofpfqfrfsftfufxfyfzg0g1dhdidjg7ghg9gmg8gagbgcgdgggigjgkglgngpgrgqgwhph4ekh3gsgtgugvgxgygzh2h5h6h7hahjhbhei4ho90hce7hkhlgfksg4g5g6gegoh0h1h8h9hghhhdhfhihqhuhshvhti5j4kakgg3i9kohmhnhrhyg2hwhxhzi0i1i2i3i6i8ifiiiji7j8iqkvikldihleirlfioliinljitllj6lmiblnizlpiglqiulsjaluixlxicillyiaiem3jkktkumfmgm5imipisiviyj7jciwkkjfm4jem8jim9jpmajbmbj5mcjqmdjnmejomhjhmijwmkk7mmjrmojlmsj0j2muj1j3mvkllblcmqmrmtj9jdjgjmjsjzjjk1k9mwk2mxk6mykhmzkmn0jxn2kqn3kdn4kfn5k3n6jyn7l1n8kcn9l7najvk0nbjtjunck4m0m1m6m7n1k5k8kbkeknkil8ndl2nel0nfkrngkxnhkpnilrnjl6nklanll3nml9nnlznolonpltnqkykznrkwl5nskjlglhlvm2mnidlwl4mllkmjmpnvnwo0o2o5o8oantnunxnynzo1o3o4o6o7o9ocobofoeodoiojokohogolomon")
+
+
 def plan(T, topo, q):
     me = T.cores[q]
     dsts = [(q + i) % 8 for i in range(1, 8)]
     direct = [d for d in dsts if topo.may_write(me, T.cores[d])]
     eo = topo.engines(me, T.cores[direct[0]])
-    zdir = direct[:(len(eo) - len(direct)) // 2]
+    zdir = direct
     free = [c for c in topo.cores_of(me) if c != me]
     rl = {}
     for d in sorted([d for d in dsts if d not in zdir], key=lambda d: d in direct):
@@ -75,7 +83,7 @@ def relay_program(g, core, T, topo, q, d, cross):
     h = len(es) // 2
     S = T.sem
     rid, pid = topo.addr(dc, core)
-    zl = T.zl[:, 128 * q:128 * q + 128] if q < 4 else T.lz[q - 4]
+    zl = T.zl[:, 128 * q:128 * q + 128] if q < 4 else T.lz[q]
     if not cross:
         g.wait_ge(S.r1, 1)
         g.remote_dma(zl, T.rz[:], S["az%d" % q], S.loc, pid, rid, emask(es))
@@ -239,8 +247,6 @@ def rank_program(g, core, T, topo):
     dma("s", "d12", whole("sz"), T.z[:], 3.0)
     dma("s", "d1", r("nt", p=(0, 64)), T.n0[me, :])
     dma("a", "d2", r("mk"), T.x0[g0:g1, :])
-    if me < 4:
-        dma("a", "d4", r("zl", 128 * me, 128 * me + 128), T.z[g0:g1, :])
     dma("s", "d3", whole("li", T.li[me, 0:96, :]), T.nx[3 * me:3 * me + 3, :])
     dma("a", "d3", whole("li", T.li[me, 96:128, :]), T.uu[g0:g1, 64:128])
     dma("s", "d13", whole("lh", T.lh[me, 0:64, :]), T.hyp[g0:g1, :])
@@ -259,17 +265,17 @@ def rank_program(g, core, T, topo):
     for i, d in enumerate(zdir):
         j = len(direct) + 2 * i
         tz.append(xfer(topo, core, T.cores[d], eo[j:j + 2], S["az%d" % me], T.sz[d],
-                       T.zl[:, 128 * me:128 * me + 128] if me < 4 else T.lz[me - 4]))
-    sent = remote(lambda: g.remote_dma_fused(tz, local_sem=S.loc), len(tz) + len(zdir), [whole("sz")], [sent])
+                       T.lz[me]))
+    sent = remote(lambda: g.remote_dma_fused(tz, local_sem=S.loc), len(rl) + len(eo) - len(direct), [whole("sz")], [sent])
     ain, nout, late = 0, 0, {me: 0}
     for q in range(8):
         if q != me:
             dq_, zq, rq = plans[q][:3]
             n = len(topo.engines(rq[me], core)) if me in rq else 0
             late[q] = 1 if me in zq else 2
-            arrive("az%d" % q, 2 if me in zq else n if me in dq_ else n // 2,
-                   r("zl", 128 * q, 128 * q + 128) if q < 4 else (None, [("lz", q, q + 1)]),
-                   4.2 if me in zq else 5.6, [sent])
+            arrive("az%d" % q, len(plans[q][3][len(zq) + 2 * zq.index(me):][:2]) if me in zq else n // 2,
+                   (None, [("lz", q, q + 1)]) if me in zq or q >= 4 else r("zl", 128 * q, 128 * q + 128),
+                   3.2 if me in zq else 5.6 if q < 4 else 4.8, [sent])
             ain += 1 if me in dq_ else n // 4
             nout += 2 if me in dq_ else n
     arrive("ain", ain, (None, [("li", 1 << 30, 1 << 31)]), 5.0, sends[1:])
@@ -403,10 +409,14 @@ def rank_program(g, core, T, topo):
     late[8] = 0
     for q in range(4, 8):
         dma("s", "d23", (T.dz[:, 1024 * q - 4096:1024 * q - 3072], [("dz", 0, 1)]),
-            T.z[g0:g1, :] if q == me else (T.lz[q - 4], [("lz", q, q + 1)]), 2.3, () if q == me else group["d6"])
+            T.z[g0:g1, :] if q == me else (T.lz[q], [("lz", q, q + 1)]), 2.3, () if q == me else group["d6"])
     for a in range(8):
         dma("s", "d24", r("Z1", 0, 4096, p=(16 * a, 16 * a + 16)), whole("dz"), 4.4)
-    for i, q in enumerate(sorted([q for q in late if q // 4 != 1], key=lambda q: late[q])):
+    for q in sorted([q for q in range(4) if late[q] < 2], key=lambda q: late[q]):
+        for a in range(8):
+            dma("sa"[a % 2], "d4", r("Z0", 1024 * q, 1024 * q + 1024, p=(16 * a, 16 * a + 16)),
+                T.z[g0:g1, :] if q == me else (T.lz[q], [("lz", q, q + 1)]), 3.2)
+    for i, q in enumerate([8] + [q for q in range(4) if late[q] == 2]):
         pa, pb = (("P0", "P1"), ("P2", "P3"), ("P6", "P7"))[i % 3]
         for ch in range(8):
             mm(r((pa, pb)[ch // 4], 128 * (ch % 4), 128 * (ch % 4) + 128), r("REP", 128 * ch, 128 * ch + 128),
@@ -424,6 +434,7 @@ def rank_program(g, core, T, topo):
     ts(r("ti", 0, 64), r("hu", 0, 64), 3, SHR)
     ts(r("ti", 64, 128), r("hu", 0, 64), 7, AND)
     cp(r("tfb"), r("ti", 0, 64))
+    ts(r("tf", 128, 192), r("ti", 64, 128), 4.0, MUL, 4096.0, ADD)
     cp(r("uz"), r("P4", 16, 40))
     cp(r("ni", 8, 32), r("P4", 16, 40))
     cp(r("ni", 40, 64), r("P4", 40, 64))
@@ -466,6 +477,7 @@ def rank_program(g, core, T, topo):
             ms(r("V", o + 3, o + 128, 4), 2.0)
         else:
             cp(r("uo0", 32 * h, 32 * h + 32), r(pb, 3, 128, 4))
+            tt(r("tf", 64 + 32 * h, 96 + 32 * h), r(pb, 131, 256, 4), r("tf", 128 + 32 * h, 160 + 32 * h), ADD)
         act(r("D", o, o + 128), r(pb, 256, 384))
         act(r("N", o, o + 128), r(pb, 128, 256))
     for h in range(2):
@@ -482,9 +494,11 @@ def rank_program(g, core, T, topo):
         ts(r("A", 128 * c, 128 * c + 128), r("iob"), r("tfb", c, c + 1), EQ)
 
     part[0] = 2
-    act(r("mk1", 512, 1024), ind(r("MB"), r("ucb", 96, 128)))
-    tt(r("G1", 512, 1024), ind(r("nxw", 1024, 2048), r("ucb", 32, 64)), r("mk1", 512, 1024), MUL)
     for m in range(4):
+        if m % 2 == 0:
+            a, b = 512 + 128 * m, 768 + 128 * m
+            act(r("mk1", a, b), ind(r("MB"), r("ucb", 96 + 8 * m, 112 + 8 * m)))
+            tt(r("G1", a, b), ind(r("nxw", 1024, 2048), r("ucb", 32 + 8 * m, 48 + 8 * m)), r("mk1", a, b), MUL)
         mm(r("P6", 24 * m, 24 + 24 * m), r("G1", 512 + 128 * m, 640 + 128 * m), r("SEL"))
     act(r("t96"), r("P6", 0, 96))
     cp(r("uz1"), ind(r("t96"), r("offc", 16, 22)))
@@ -501,18 +515,18 @@ def rank_program(g, core, T, topo):
                r("tm", 128 * j, 128 * j + 128), False, False)
     for m in range(4):
         mm(r("P7", 128 * m, 128 * m + 128), r("LN"), r("G1", 128 * m, 128 * m + 128), False, False)
-    for m in range(3):
-        a, b = 512 * m, 512 * m + 512
-        tt(r("d1g", a, b), ind(r("Z1", 0, 4096), r("uz1", 32 * m, 32 * m + 32)), r("xn"), SUB)
+    for a, b in ((0, 512), (512, 1024), (1024, 1280), (1280, 1536)):
+        m, c = a // 512, a % 512
+        tt(r("d1g", a, b), ind(r("Z1", 0, 4096), r("uz1", a // 16, b // 16)), r("xn", c, c + b - a), SUB)
         act(r("ab", a, b), r("d1g", a, b), ACT.Abs)
         ts(r("near", a, b), r("ab", a, b), 1.0, LE_)
-        mm(r("P7"), r("LW", 128 * m, 128 * m + 128), r("near", a, b), False, m == 2)
+        mm(r("P7", c, c + b - a), r("LW", 128 * m, 128 * m + 128), r("near", a, b), False, b == 1536)
     act(r("tm"), r("P7"), scale=lomask)
     tt(r("tb"), r("P7"), r("tm"), SUB)
     for q in range(8):
-        dma("s", "d9", whole("dt", T.dt[:, 512 * q:512 * q + 512]), r("tb", p=(16 * q, 16 * q + 16)), 2.4)
+        dma("sa"[q % 2], "d9", whole("dt", T.dt[:, 512 * q:512 * q + 512]), r("tb", p=(16 * q, 16 * q + 16)), 2.4)
     for a in range(8):
-        dma("s", "d10", r("tab1", p=(16 * a, 16 * a + 16)), whole("dt"), 4.4)
+        dma("sa"[a % 2], "d10", r("tab1", p=(16 * a, 16 * a + 16)), whole("dt"), 4.4)
 
     def draw(t, k):
         o = 256 * t + 64 * k
@@ -557,14 +571,12 @@ def rank_program(g, core, T, topo):
     q = (me + 1) % 8
     arrive("win", len(topo.engines(T.cores[q] if me in plans[q][0] else plans[q][2][me], core)), r("ein"), 5.5, [sent])
     for k in range(4):
-        act(r("fe", 256 * k, 256 * k + 256), ind(r("tab1"), r("uo1", 32 * k, 32 * k + 16)))
+        (cp if k % 2 else act)(r("fe", 256 * k, 256 * k + 256), ind(r("tab1"), r("uo1", 32 * k, 32 * k + 16)))
     for h in range(2):
         fields(h)
         evac(1, h)
         act(r("xr", 512 * h, 512 * h + 512), ind(r("Z0", 4096, 5120), r("uh", 32 * h, 32 * h + 32)))
         act(r("zr", 512 * h, 512 * h + 512), ind(r("Z0"), r("uo0", 32 * h, 32 * h + 32)))
-    ts(r("tf", 128, 192), r("ti", 64, 128), 4.0, MUL, 4096.0, ADD)
-    tt(r("tf", 64, 128), r("tf", 128, 192), r("N", 259, 512, 4), ADD)
     ts(r("tf", 192, 256), r("tfb"), 32.0, MUL)
     tt(r("tf", 192, 256), r("tf", 192, 256), r("tf", 64, 128), ADD)
     act(r("tf", 64, 128), r("tf", 64, 128), scale=4.0)
@@ -614,7 +626,11 @@ def rank_program(g, core, T, topo):
         scan(r("O1", 64 * k, 64 * k + 64), c, r("PAT", 512 + 64 * k, 576 + 64 * k))
         cp(r("ut1", 16 * k, 16 * k + 16), r("TK", 256 + 64 * k + 3, 256 + 64 * k + 64, 4))
         for c in range(16 * k, 16 * k + 16):
-            ts(r("Bm", 128 * c, 128 * c + 128), r("iob"), r("O1", 4 * c + 3, 4 * c + 4), EQ)
+            if c % 16 < 14:
+                ts(r("Bm", 128 * c, 128 * c + 128), r("iob"), r("O1", 4 * c + 3, 4 * c + 4), EQ)
+            else:
+                act(r("ab", 128 * (c % 8), 128 * (c % 8) + 128), r("iob"), ACT.Abs, -1.0, r("O1", 4 * c + 3, 4 * c + 4))
+                act(r("Bm", 128 * c, 128 * c + 128), r("ab", 128 * (c % 8), 128 * (c % 8) + 128), ACT.Relu, -1.0, r("ONF", 0, 1))
             mm(r("P6", 0, 128), r("A", 128 * c, 128 * c + 128), r("Bm", 128 * c, 128 * c + 128), c == 0, c == 63)
         a, b = 256 * k, 256 * k + 256
         act(r("ue", a, b), ind(r("Z1"), r("ut1", 16 * k, 16 * k + 16)))
@@ -656,7 +672,7 @@ def rank_program(g, core, T, topo):
                 for j, d in enumerate([d for d in rl if d not in direct])]
         sent = remote(lambda tr_=tr_: g.remote_dma_fused(tr_, local_sem=S.loc), 2 * len(tr_), [whole(st)])
         arrive(so, nout, (None, [(ld, 1, 2)]), 5.0, [sent])
-        dma("s", "d%d" % (18 + 3 * i), out[:], whole(ld))
+        dma("sa"[i], "d%d" % (18 + 3 * i), out[:], whole(ld))
 
     n = len(ops)
     succ = [[] for _ in range(n)]
@@ -678,13 +694,9 @@ def rank_program(g, core, T, topo):
     val = [0] * n
     known = {e: {} for e in Q}
     for _ in range(n):
-        t0, e = min((max(free[e], min(ready[i] for i in c)), e) for e, c in cand.items() if c)
-        now = [i for i in cand[e] if ready[i] <= t0]
-        i = max(now, key=lambda i: prio[i])
-        soon = [j for j in cand[e] if t0 < ready[j] < t0 + 0.6 * ops[i][4] and prio[j] > prio[i] + 1.0]
-        if soon:
-            i = min(soon, key=lambda j: ready[j])
-        cand[e].remove(i)
+        i = min((j for c in cand.values() for j in c), key=lambda j: int(ORDER[2 * j:2 * j + 2], 36))
+        t0 = 0.0
+        cand[ops[i][0]].remove(i)
         e, fn, sem, inc, busy, lat, pre = ops[i][:7]
         t0 = max(t0, ready[i])
         free[e] = t0 + busy

from concourse.bass import DstId, RemoteDMATransfer
from concourse.mybir import AluOpType as ALU, AxisListType, ActivationFunctionType as ACT

F, B, I, U = "float32", "bfloat16", "int32", "uint16"
SB = {
    "zl": (1152, B), "Z0": (5120, B), "Z1": (4112, B), "nxw": (2048, I), "hu": (192, I),
    "nt": (16, I), "nf": (16, F), "pint": (8, I), "pc": (24, B), "pf": (16, F), "colf": (128, B), "colq": (128, B),
    "tmpd": (256, B), "cod": (64, B), "REP": (1024, B), "PERM": (128, B),
    "RQ": (1024, B), "TRI": (128, B), "ONE": (1024, B), "ONF": (128, F), "IQ": (512, B), "iob": (128, B), "LW": (384, B),
    "LN": (128, F), "LE": (1024, B), "CR": (768, B), "RW": (96, B), "R8": (8, B), "SEL": (24, F), "RN8": (16, F), "MB": (8, F),
    "MN": (256, B), "LL": (256, F), "offc": (80, U), "offf": (80, F), "mrow": (512, B), "WL": (32, B), "ulut": (64, F),
    "elut": (48, F), "RM": (64, F), "ni": (64, I), "nb": (128, I), "ucb": (128, U), "uc0": (32, U), "uz": (24, U), "uz1": (96, U),
    "G0": (256, F), "mk1": (1024, F), "G1": (1024, F), "xg": (384, F), "xn": (512, F), "t96": (96, F),
    "d0g": (384, F), "dq": (384, F), "ab": (1536, B), "near": (1536, B), "d1g": (1536, F), "tm": (512, B), "tb": (512, B),
    "tab0": (1024, B), "tab1": (4096, B), "fe": (1024, B), "ue": (1024, B), "uh": (128, U), "tf": (384, F), "ti": (256, I),
    "tfb": (64, B), "A": (8192, B), "Bm": (8192, B), "V": (512, F), "N": (512, F), "D": (512, F), "ub": (128, F), "R": (512, F),
    "tt": (256, F), "cb": (528, F), "TK": (512, F), "ne": (192, F), "PAT": (768, F), "O0": (512, F), "O1": (256, B),
    "uo1": (128, U), "mE": (1024, B), "mk": (128, F), "inc": (128, B), "cmp": (128, B), "th": (8, F), "sm": (640, F),
    "ecol": (4, F), "ein": (4, F), "uo0": (64, U), "ut1": (64, U), "xr": (1024, B), "zr": (1024, B), "x1q": (1024, F),
    "xw": (2056, F), "d1": (1024, F), "ad": (1024, F), "ex0": (1024, F), "uf": (96, U), "ye_s": (256, F), "yx_s": (256, F),
}
SCRATCH = {k: ("sbuf", [128, n], t) for k, (n, t) in SB.items()}
SCRATCH.update({"P%d" % i: ("psum", [128, 512], F) for i in range(8)})
SCRATCH.update({
    "sz": ("dram", [8, 128, 128], B), "si": ("dram", [8, 128, 32], I), "li": ("dram", [8, 128, 32], I),
    "sh": ("dram", [8, 128, 16], I), "lh": ("dram", [8, 128, 16], I), "rh": ("dram", [128, 16], I),
    "rz": ("dram", [128, 128], B), "ri": ("dram", [128, 32], I), "rw": ("dram", [128, 1], F),
    "lz": ("dram", [8, 128, 128], B), "dz": ("dram", [16, 4096], B),
    "dt": ("dram", [16, 4096], B), "se": ("dram", [8, 128, 32], F), "sx": ("dram", [8, 128, 32], F),
    "le": ("dram", [8, 128, 32], F), "lx": ("dram", [8, 128, 32], F), "re_": ("dram", [128, 32], F), "rx": ("dram", [128, 32], F),
})
SEMAPHORES = (["sv", "sa", "sp", "sg", "loc", "ain", "win", "oe", "ox", "ah", "r1", "r2", "r3", "r4", "r5", "r6"] + ["az%d" % i for i in range(8)]
              + ["d%d" % i for i in range(25)])


AHEAD = {"^vxw5": 5, "^aZ00": 6.4, "^vZ00": 5, "^gex04": 6, "^vye_s6": 1, "vsm6": -2.3, "^vth6": 5.3, "vxw5": -7.5, "vV5": 3,
         "^ssx6": 1.5, "^vPAT4": 6, "vecol3": 3.7, "vtf6": 0.8, "vuf6": -7.5, "^aN4": 6, "^pP31": -6, "pP20": -6, "^vTK5": 0.7,
         "^pP41": -1.5, "^vRW0": 3, "^vR5": 0.8, "vd16": 1.5, "^vO15": 0.7, "^pP70": 3, "^aue1": 3, "^vne3": -0.7, "^vO03": 3.0,
         "^vCR0": 1.5, "^pP13": 0.7, "pP00": 1.5, "^pP01": 1.5, "vpc0": -6, "vO15": -0.7, "vni1": 6, "^gRQ0": -6, "vtmpd0": -6,
         "pP01": -6, "^vuc00": -5.3, "vnf0": -3, "^pP34": -1.5, "^pP44": 0.7, "vtm1": -3, "vTK3": 6, "pP14": 6}


AHEAD.update({"vxw5": 0, "pP20": -6.7, "vd16": -4.5, "^vO15": 0, "vpc0": 0, "vO15": 0, "vtmpd0": 0, "vnf0": 0, "^aue5": 3, "pP60": 6,
              "^atm2": -0.7, "vTK5": -3, "aue1": -3, "^vMN0": -3, "^vuf6": 0.7, "vCR0": 3, "^sdz0": -3, "vth6": -3, "^velut0": -6,
              "^vLE0": -0.7, "^vcmp6": -6, "vne5": 1.5, "^vpf0": 6, "^aD1": 0.7, "^vtt5": 0.7})


ORDER = (
    "03020605080c090a070o0m0v1u22252627282f2i2e231g000u0j0t2q013x413g643h5v494d3k5w4b3w0r0w0q0s0e0p0f0x045h5z4v3r5x6saz181314291o1s1k1p1m1w1c2u0z151b1i171e1f1j1h1n2v2x2y3m3o1r2b1v242h2c2j202l0y19103j4g5p1112161a4a2m371d3q3e774t7c4x5k1l2g2k2o42464o443t3u333d742s2r2w2t302z313b34383l3a353c3f3i4e3y4w2n48el3s3v365m405n7p432p45ft6e797g4s534h513z524c4u897q7a7e7n83877r3p3nam9k9n9m9l9za3a59ya0a1a4a20g0b0i0d0l0h0n0k5i5f6t586k5d68555j5c6n5666546a5969575y5e625b6j5a1y2a2d321q1t1x1z39215q60634k4i4f4l4jeg6l6m6o6u6y7h6x6w6z715t6b6p6q6r6v7576787j7k7l7m7x7o7z80818d828j8s9b9r8k8l8m8n8o8p8t8u8v8w8x9091929j9a9p9q9c9d9e9f9g9h9s9t9u9v9w9xagafahbdatasaqav5g5r6f6g6h6i72737b8485c34n5l7s67657u5obpccbe5scscgd086d5d84m6c7tc94y50ct88dwdme5due2do4z5ue8ds7ieh7ye6dbe0edebeteee3eaek7df3fieoejeueneserdvfue9e7frfs708a8b8c7w8g8h8i8y8z8r7v8q474p4q4r6d7f8e8f939495969899a6a8a9aba7acadaiaaajakanaeaoapawaxb4bcbob5bsb6brb7bgbwcybtcnbucrbvcz9i9oalarayb1bhaub0b2b8babbbyc4c5c6c7cacbcecfcjckcmcqcvcwd3d4b3b9bfbibkbmc0blbjbnbxbzc2cld6d9dadddedfdgdhdidxdye1efeqevewbqc1c8cdcicpchcocxd2dpdze4exeyezf0f1f2f4f5f6f8f9fafbfcfdfecud1d7dkdjdqdremepf7fffgfhfjfkflfmfnfofpfqfvfwfxfyfzdcdldng8g5gagig9gbgcgegfggghgkglgmgngogygpgqh8hm61grgsgtgugvgwgxgzh0h1h2h3h4hgh9h5hyhl97hieihahbecmmg0g1g2g3g4gdgjh6h7hehfhchdhjhohphnhzhki1ixiyjsg7ieiuhhhqhrhug6hshthvhwhxi0i2i3i4i6i8ici5j6ifj1ikklinkmilknijkoiskpiwkqirkriqksj4ktigkuj9kvi7kwipkxiaiikyi9ibkzjek5kdmsmvmaidihimioitj0jfivkejdl0jil1jgl2j3l3jjl4j2l5jml6jll7jrl8jql9k0lajblbjylcjzleizj8loj7jalukim6m8m9mgnij5jcjhjkjnjpjokgk7lvkalykbm3k9m5kjmfk2mhlgmlk4mnkkmplpmrlhmwlkmxldmyk6n0jwjxn1jujvn2khm0m1mcmjnljtk1k3k8lfkclzn6lrn7m4n8lqn9lmnbmbncmdndlxnemenfm7ngmunhmtnjmonkminnlilnnoljlwnpkflsltmkmqmzdtnam2n4lln3n5nmnsnwnyo0o4o6nqnrntnunvnxnzo1o2o3o5obocodo8o7o9oaogofoeohoioj")


ORDER = (
    "03020605080b090a070g0f1j1t202324254r2c2f2b211k000m0e0l2o013r3w3e693b5m4a4d3g5n3u3p0j0n0i0k0c0h0d0o044l624h3jad9nau0z0u0v261e1q1a1n1c1v131f0q0w12180y151619171d1g1h1i1l1m1p281u222e292g1z5b0p100r3d4c5p0s0t0x11472j31143i397i617j4i641b2d2h2l3y453l433m3n2x387c2q2p2s2r2u2t2v342y323h332z353a3c4e50562k46ee3k3o304q3s4v8y3z2n44ez6t7h7m5t4t5258575a5s4y807z7u68747e6j751s40ab799o919p9s9q9t9r9w9x9v9u48364u3f414b3x373v426k4f2i3t2m3q1x272a2w1o1r1w1y6h5e4m4n4o4z5f5g5h5i5o60595k5q5v4s545c5d5x5y5w63654p4j4g494kfw66676e6l6z776r6s6x706i6u6q6v6w6y7172767o7q7v7w7y7r7s7t818d828g8n989f8h8i8j8k8l8m8o8p8q8r8s8z9ka2aja1akal999a9b9c9d9e9g9h9i9j9l9maianambiasaravax6c5j6f6g6m6n6p787d7l86bx4x537xc0877n4wclc8bn8uc3cicy7gbpd7555184b25u5rdocgdvdde3dte4dn5le2ecdu7feg8te0elebeaedepe6eie9ej73ereueneheqefeoesdwfvete8exey7a888a8b7b898c8e8w8x8v7p8f5z6a6b6d6o7k83859293949596979ya3a6a8a0a5aaac9za4afaha9aeapaqatb8bgbfbbbdbcbabeb9bwd2btd9bucpbvd1a7agaoawayb1bkazb0b3b5b6b7byc4c5c6c7c9cacecfcqcrcvcwcxczd3d4b4bhbjblbobrccbmbqbsc1ckcncod5d8dbdcdedfdgdkdpdxdye1emewf0f1bzc2cbcdchcjctcsd0dadqdze5f2f3f6f7f8f9fafbfcfdfefffgfhfifjcmcud6dmdldrdsevf4f5fkflfmfnfofpfqfrfsftfufxfyfzg0g1dhdidjg7ghg9gmg8gagbgcgdgggigjgkglgngpgrgqgwhph4ekh3gsgtgugvgxgygzh2h5h6h7hahjhbhei4ho90hce7hkhlgfksg4g5g6gegoh0h1h8h9hghhhdhfhihqhuhshvhti5j4kakgg3i9kohmhnhrhyg2hwhxhzi0i1i2i3i6i8ifiiiji7j8iqkvikldihleirlfioliinljitllj6lmiblnizlpiglqiulsjaluixlxicillyiaiem3jkktkumfmgm5imipisiviyj7jciwkkjfm4jem8jim9jpmajbmbj5mcjqmdjnmejomhjhmijwmkk7mmjrmojlmsj0j2muj1j3mvkllblcmqmrmtj9jdjgjmjsjzjjk1k9mwk2mxk6mykhmzkmn0jxn2kqn3kdn4kfn5k3n6jyn7l1n8kcn9l7najvk0nbjtjunck4m0m1m6m7n1k5k8kbkeknkil8ndl2nel0nfkrngkxnhkpnilrnjl6nklanll3nml9nnlznolonpltnqkykznrkwl5nskjlglhlvm2mnidlwl4mllkmjmpnvnwo0o2o5o8oantnunxnynzo1o3o4o6o7o9ocobofoeodoiojokohogolomon")


def plan(T, topo, q):
    me = T.cores[q]
    dsts = [(q + i) % 8 for i in range(1, 8)]
    direct = [d for d in dsts if topo.may_write(me, T.cores[d])]
    eo = topo.engines(me, T.cores[direct[0]])
    zdir = direct
    free = [c for c in topo.cores_of(me) if c != me]
    rl = {}
    for d in sorted([d for d in dsts if d not in zdir], key=lambda d: d in direct):
        ok = [c for c in free if c not in rl.values() and topo.may_write(c, T.cores[d])]
        rl[d] = min(ok, key=lambda c: (sum(topo.may_write(c, T.cores[e]) for e in dsts), topo.die(c) != topo.die(me)))
    rest = [e for e in topo.engines(me, free[0]) if e not in eo]
    return direct, zdir, rl, eo, rest


def emask(es):
    return sum(1 << e for e in es)


def xfer(topo, src, dst, es, sem, a, b):
    rid, pid = topo.addr(dst, src)
    return RemoteDMATransfer(dst_ids=[DstId(rid=rid, pnc=pid)], dma_engine_mask=emask(es), remote_sem=sem, src=a, dst=b)


def relay_program(g, core, T, topo, q, d, cross):
    dc = T.cores[d]
    es = topo.engines(core, dc)
    h = len(es) // 2
    S = T.sem
    rid, pid = topo.addr(dc, core)
    zl = T.zl[:, 128 * q:128 * q + 128] if q < 4 else T.lz[q]
    if not cross:
        g.wait_ge(S.r1, 1)
        g.remote_dma(zl, T.rz[:], S["az%d" % q], S.loc, pid, rid, emask(es))
        g.wait_ge(S.loc, len(es))
        return
    g.wait_ge(S.r5, 1)
    g.remote_dma(T.lh[q], T.rh[:], S.ah, S.loc, pid, rid, emask(es[:h // 2]))
    g.wait_ge(S.r6, 1)
    g.remote_dma(T.li[q], T.ri[:], S.ain, S.loc, pid, rid, emask(es[h // 2:h]))
    g.wait_ge(S.r1, 1)
    g.remote_dma(zl, T.rz[:], S["az%d" % q], S.loc, pid, rid, emask(es[h:]))
    n = 3 * len(es)
    if d == (q - 1) % 8:
        g.wait_ge(S.r2, len(topo.engines(T.cores[q], core)))
        g.remote_dma(T.ein[:, 0:1], T.rw[:], S.win, S.loc, pid, rid, emask(es))
        n += len(es)
    g.wait_ge(S.r3, 2)
    g.remote_dma(T.le[q], T.re_[:], S.oe, S.loc, pid, rid, emask(es))
    g.wait_ge(S.r4, 2)
    g.remote_dma(T.lx[q], T.rx[:], S.ox, S.loc, pid, rid, emask(es))
    g.wait_ge(S.loc, n)


def rank_program(g, core, T, topo):
    rank = T.rank_of(core)
    if rank is None:
        for q in range(len(T.cores)):
            if core in topo.cores_of(T.cores[q]):
                direct, zdir, rl, eo, rest = plan(T, topo, q)
                for d, c in rl.items():
                    if c == core:
                        relay_program(g, core, T, topo, q, d, d not in direct)
        return
    me = rank
    S = T.sem
    plans = [plan(T, topo, q) for q in range(8)]
    direct, zdir, rl, eo, rest = plans[me]
    Q = {"v": g.vector, "a": g.scalar, "p": g.tensor, "g": g, "s": g.sync}
    ops = []
    recs = {}
    group = {}
    part = [0]
    CY = 0.00104

    def r(name, a=None, b=None, st=1, p=None):
        t = T[name]
        if a is None:
            a, b = 0, t.shape[-1]
        ps = slice(0, 128) if p is None else slice(p[0], p[1])
        two = name in SB and SB[name][1] in (B, U)
        return (t[ps, a:b:st] if st != 1 else t[ps, a:b], [(name, a, b)], (b - a + st - 1) // st, two, name not in SB, False)

    def ind(w, o):
        return (w[0].indirect(o[0]), w[1] + o[1], 16 * o[2], False, False, True)

    def whole(name, ap=None):
        return (T[name][:] if ap is None else ap, [(name, 0, 1 << 30)])

    def regs(xs):
        return [y for x in xs if isinstance(x, tuple) for y in x[1]]

    def ap(x):
        return x[0] if isinstance(x, tuple) else x

    def add(e, fn, sem, inc, busy, lat, outs, ins, after=()):
        me_ = len(ops)
        pre = {x: False for x in after}
        dm = sem[0] != "s"
        for rs, wr in ((regs(ins), False), (regs(outs), True)):
            for (n, a, b) in rs:
                ps = n[0] == "P" and n[1:].isdigit()
                for (a2, b2, o2, w2) in recs.get(n, []):
                    e2, s2 = ops[o2][0], ops[o2][2]
                    if dm and s2 == sem:
                        continue
                    if ps and e == "p" and e2 == "p":
                        pre.setdefault(o2, False)
                    elif (ps and e2 != e) or (a < b2 and a2 < b and (wr or w2)):
                        for o3 in group.get(s2, [o2]):
                            pre[o3] = True
        for rs, wr in ((regs(ins), False), (regs(outs), True)):
            for (n, a, b) in rs:
                l = recs.setdefault(n, [])
                if wr:
                    l[:] = [x for x in l if not (a <= x[0] and x[1] <= b and pre.get(x[2]))]
                l.append((a, b, me_, wr))
        if dm:
            group.setdefault(sem, []).append(me_)
        ops.append([e, fn, sem, inc, busy, lat, pre, e + "".join(x[0] for x in regs(outs)[:1]) + str(part[0])])
        return me_

    def op(e, fn, out, ins, cost):
        return add(e, fn, "s" + e, 1, cost, cost + 0.06, [out], ins)

    def dma(e, sem, out, src, lat=2.3, after=(), **k):
        return add(e, lambda: Q[e].dma_start(ap(out), ap(src), **k), sem, 16, 1.0 if e == "g" else 0.1, lat, [out], [src], after)

    def arrive(sem, n, out, t, after=()):
        return add("x", None, sem, n, 0.0, t, [out], [], after)

    def remote(fn, n, ins, after=()):
        return add("g", fn, "loc", -n, 0.6, 0.6, [], ins, after)

    def landed(name, ap_):
        return (ap_, [(name, 0, 1 << 31)])

    def vcost(out, ins, two=False):
        if ins[0][5]:
            return 0.05 + out[2] * 1.56 * CY
        f = 0.5 if all(x[3] for x in ins + [out] if isinstance(x, tuple)) else 1.0
        if two:
            f = 1.0 if ins[0][4] or ins[1][4] else 2.0
        return max(64, max(out[2], ins[0][2]) * f) * CY

    def ts(out, a, s1, o1, s2=None, o2=None):
        if o2 is None:
            op("v", lambda: g.vector.tensor_scalar(ap(out), ap(a), ap(s1), None, o1), out, [a, s1], vcost(out, [a, s1]))
        else:
            op("v", lambda: g.vector.tensor_scalar(ap(out), ap(a), ap(s1), ap(s2), o1, o2), out, [a, s1, s2], vcost(out, [a, s1, s2]))

    def tt(out, a, b, o):
        op("v", lambda: g.vector.tensor_tensor(ap(out), ap(a), ap(b), o), out, [a, b], vcost(out, [a, b], True))

    def cp(out, a):
        op("v", lambda: g.vector.tensor_copy(ap(out), ap(a)), out, [a], vcost(out, [a]))

    def ms(out, c):
        op("v", lambda: g.vector.memset(ap(out), c), out, [], vcost(out, [out]))

    def scan(out, a, b):
        op("v", lambda: g.vector.tensor_tensor_scan(ap(out), ap(a), ap(b), 0.0, ALU.mult, ALU.add), out, [a, b], vcost(out, [a, b]))

    def red(out, a):
        op("v", lambda: g.vector.tensor_reduce(ap(out), ap(a), AxisListType.X, ALU.add), out, [a], max(64, a[2]) * CY)

    def act(out, a, f=ACT.Identity, scale=1.0, bias=0.0):
        op("a", lambda: g.scalar.activation(ap(out), ap(a), f, bias=ap(bias), scale=ap(scale)), out, [a, scale, bias],
           0.065 + out[2] * 1.56 * CY if a[5] else max(64, out[2]) * CY)

    def mm(out, l, x, st=True, sp=True):
        op("p", lambda: g.tensor.matmul(ap(out), ap(l), ap(x), st, sp), out, [l, x], max(64, x[2]) * (1 if x[3] else 4) * CY)

    def iota(out, pat, base=0, cm=0, fl=True):
        if fl:
            op("g", lambda: g.iota(ap(out), pat, base, cm, allow_small_or_imprecise_dtypes=True), out, [], 0.13 + 2 * out[2] * CY)
        else:
            op("g", lambda: g.iota(ap(out), pat, base, cm), out, [], 0.13 + 2 * out[2] * CY)

    def sel(out, a, pat, cmp_, base, cm):
        op("g", lambda: g.affine_select(ap(out), ap(a), pat, cmp_, 0.0, base, cm), out, [a], 0.17 + 2 * out[2] * CY)

    EQ, GE, LE_, LT, GT, NE = ALU.is_equal, ALU.is_ge, ALU.is_le, ALU.is_lt, ALU.is_gt, ALU.not_equal
    ADD, SUB, MUL, MAX = ALU.add, ALU.subtract, ALU.mult, ALU.max
    AND, SHR = ALU.bitwise_and, ALU.arith_shift_right
    g0, g1 = 16 * me, 16 * me + 16

    dma("s", "d0", whole("sh", T.sh[:, 0:64, :]), T.hyp[:])
    dma("a", "d0", whole("sh", T.sh[:, 64:128, :]), T.uu[:, 0:64])
    dma("s", "d11", whole("si", T.si[:, 0:96, :]), T.nx[:], 2.6)
    dma("a", "d11", whole("si", T.si[:, 96:128, :]), T.uu[:, 64:128], 2.6)
    dma("s", "d12", whole("sz"), T.z[:], 3.0)
    dma("s", "d1", r("nt", p=(0, 64)), T.n0[me, :])
    dma("a", "d2", r("mk"), T.x0[g0:g1, :])
    dma("s", "d3", whole("li", T.li[me, 0:96, :]), T.nx[3 * me:3 * me + 3, :])
    dma("a", "d3", whole("li", T.li[me, 96:128, :]), T.uu[g0:g1, 64:128])
    dma("s", "d13", whole("lh", T.lh[me, 0:64, :]), T.hyp[g0:g1, :])
    dma("a", "d13", whole("lh", T.lh[me, 64:128, :]), T.uu[g0:g1, 0:64])
    spare = eo[len(direct) + 2 * len(zdir):] + rest
    cross = [d for d in rl if d not in direct]
    sent = None
    sends = []
    for st, ld, rb, sd, sr in (("sh", "lh", "rh", "ah", "r5"), ("si", "li", "ri", "ain", "r6")):
        tr = [xfer(topo, core, T.cores[d], [eo[i]], S[sd], T[st][d], T[ld][me]) for i, d in enumerate(direct)]
        tr += [xfer(topo, core, rl[d], [spare[i]], S[sr], T[st][d], T[rb][:]) for i, d in enumerate(cross)]
        sent = remote(lambda tr=tr: g.remote_dma_fused(tr, local_sem=S.loc), len(tr), [whole(st)], sends[-1:])
        sends.append(sent)
    ops[sends[0]][4] = 2.0
    tz = [xfer(topo, core, rl[d], [spare[len(cross) + i]], S.r1, T.sz[d], T.rz[:]) for i, d in enumerate(rl)]
    for i, d in enumerate(zdir):
        j = len(direct) + 2 * i
        tz.append(xfer(topo, core, T.cores[d], eo[j:j + 2], S["az%d" % me], T.sz[d],
                       T.lz[me]))
    sent = remote(lambda: g.remote_dma_fused(tz, local_sem=S.loc), len(rl) + len(eo) - len(direct), [whole("sz")], [sent])
    ain, nout, late = 0, 0, {me: 0}
    for q in range(8):
        if q != me:
            dq_, zq, rq = plans[q][:3]
            n = len(topo.engines(rq[me], core)) if me in rq else 0
            late[q] = 1 if me in zq else 2
            arrive("az%d" % q, len(plans[q][3][len(zq) + 2 * zq.index(me):][:2]) if me in zq else n // 2,
                   (None, [("lz", q, q + 1)]) if me in zq or q >= 4 else r("zl", 128 * q, 128 * q + 128),
                   3.2 if me in zq else 5.6 if q < 4 else 4.8, [sent])
            ain += 1 if me in dq_ else n // 4
            nout += 2 if me in dq_ else n
    arrive("ain", ain, (None, [("li", 1 << 30, 1 << 31)]), 5.0, sends[1:])
    arrive("ah", ain, (None, [("lh", 1 << 30, 1 << 31)]), 6.0, sends[:1])

    iota(r("pint", 0, 1), [[0, 1]], 0, 1, False)
    iota(r("iob"), [[1, 128]])
    iota(r("colf"), [[0, 8], [1, 16]])
    iota(r("colq"), [[1, 8], [0, 16]])
    iota(r("cod", 0, 32), [[16, 8], [1, 4]])
    iota(r("cod", 32, 56), [[1, 3], [4, 8]])
    iota(r("offf", 0, 4), [[4, 4]])
    iota(r("offf", 4, 16), [[0, 3], [16, 4]], 3)
    iota(r("offf", 16, 22), [[8, 3], [48, 2]])
    iota(r("sm", 0, 64), [[16, 64]], 8)
    iota(r("mrow"), [[1, 4], [0, 128]])
    iota(r("tt"), [[0, 256]], 1000000)
    iota(r("PAT", 0, 256), [[0, 256]], 128)
    iota(r("PAT", 256, 768), [[0, 512]], 1)
    iota(r("WL"), [[1, 16], [0, 2]])
    iota(r("elut"), [[1, 6], [1, 8]])
    iota(r("t96", 0, 48), [[1, 6], [0, 8]])
    iota(r("ONF"), [[0, 128]], 1)

    for j, (s, o) in enumerate(((3, SHR), (7, AND), (4, SHR), (15, AND), (3, AND), (12, AND), (8, AND))):
        ts(r("pint", j + 1, j + 2), r("pint", 0, 1), s, o)
    cp(r("pc", 0, 8), r("pint"))
    p_, p3, p7, p4, pf, pm, p12, p8 = [r("pc", j, j + 1) for j in range(8)]

    def pcol(j):
        return r("pc", j, j + 1)
    ms(r("ONE"), 1.0)
    sel(r("RQ"), r("ONE"), [[-16, 8], [0, 8], [-1, 16]], EQ, 0, 1)
    sel(r("TRI"), r("ONE", 0, 128), [[1, 128]], GT, 0, -1)
    sel(r("IQ", 0, 128), r("ONE", 0, 128), [[-1, 128]], EQ, 0, 1)
    sel(r("R8"), r("ONE", 0, 8), [[-16, 8]], EQ, 0, 1)
    for j, c in enumerate((-1.0, 0.25, 0.75)):
        act(r("IQ", 128 * j + 128, 128 * j + 256), r("IQ", 0, 128), scale=c)
    ms(r("nt", p=(64, 128)), 0)
    ts(r("inc"), r("colf"), 8.0, MUL)
    for ch in range(8):
        ts(r("REP", 128 * ch, 128 * ch + 128), r("inc"), float(ch), ADD, p_, EQ)
    cp(r("zl", 1024, 1152), r("mk"))
    sel(r("PERM"), r("ONE", 0, 128), [[-1, 8], [-8, 16]], EQ, 0, 1)
    ts(r("MN", 0, 128), r("colq"), p7, EQ)
    ts(r("MN", 128, 256), r("colq"), p3, EQ)
    ts(r("RN8", 0, 8), r("iob", 0, 8), p3, EQ)
    ts(r("RN8", 8, 16), r("iob", 0, 8), p7, EQ)
    ts(r("offc", 56, 64), r("iob", 0, 8), 0.0, MUL, pf, ADD)
    cp(r("nf"), r("nt"))
    for j in range(2):
        tt(r("LL", 128 * j, 128 * j + 128), ind(r("nf"), r("offc", 56, 64)), r("MN", 128 * j, 128 * j + 128), MUL)
        mm(r("P4", 8 * j, 8 * j + 8), r("LL", 128 * j, 128 * j + 128), r("RN8", 8 * j, 8 * j + 8))
    for j in range(3):
        mm(r("P5", 128 * j + 128, 128 * j + 256), r("PERM"), r("zl", 1024, 1152))
    act(r("xg"), r("P5", 128, 512))
    act(r("xn", 0, 128), r("P5", 128, 256))
    cp(r("ni", 32, 40), r("P4", 0, 8))
    cp(r("ni", 0, 8), r("P4", 8, 16))
    for j, c in ((0, 32), (1, 0)):
        ts(r("nb", 8 * j, 8 * j + 8), r("ni", c, c + 8), 1023, AND)
        ts(r("nb", 16 + 8 * j, 24 + 8 * j), r("ni", c, c + 8), 10, SHR)
    cp(r("uc0"), r("nb", 0, 32))
    ts(r("MB"), r("iob", 0, 8), 4.0, MUL, p12, EQ)
    act(r("mk1", 0, 256), ind(r("MB"), r("uc0", 16, 32)))
    ts(pcol(8), p4, 4.0, MUL, pm, ADD)
    ts(r("SEL"), r("cod", 32, 56), pcol(8), EQ)
    ts(pcol(9), p4, 16.0, MUL)
    for m in range(3):
        ts(r("LW", 128 * m, 128 * m + 128), r("iob"), float(m - 2), ADD, pcol(9), EQ)
    ts(pcol(10), pm, 3.0, EQ, 500.0, MUL)
    ts(pcol(11), pm, -8.0, ADD, pcol(9), SUB)
    ts(r("pf", 0, 1), pcol(11), pcol(10), ADD)
    act(r("cmp"), r("iob"), ACT.Abs, 1.0, r("pf", 0, 1))
    ts(r("LN"), r("cmp"), 2.0, EQ)
    ts(r("pc", 21, 24), r("iob", 0, 3), pm, NE, 500.0, MUL)
    ts(r("pc", 21, 24), r("pc", 21, 24), pcol(9), ADD)
    ts(pcol(12), r("pf", 0, 1), -1.0, MUL)
    for j in range(2):
        for m in range(3):
            ts(r("LE", 384 * j + 128 * m, 384 * j + 128 * m + 128), r("iob"), -12.0 - j, ADD, pcol(21 + m), EQ)
        ts(r("LE", 768 + 128 * j, 896 + 128 * j), r("iob"), 2.0 - 4 * j, ADD, pcol(12), EQ)
    ms(r("CR"), 0.0)
    for c, v in ((11, 1.0), (14, 1.0), (128 + 14, 1.0), (256 + 7, 4096.0), (640 + 15, 1.0)):
        ms(r("CR", c, c // 128 * 128 + 128, 16), v)
    ts(r("CR", 384 + 12, 512, 16), r("iob", 0, 8), 128.0, MUL, 4096.0, ADD)
    ts(r("CR", 512 + 7, 640, 16), r("iob", 0, 8), 128.0, MUL, 4096.0, ADD)
    ts(r("CR", 512 + 12, 640, 16), r("iob", 0, 8), 512.0, MUL)
    ts(pcol(15), pf, 7.5, GT, pf, MUL)
    ts(pcol(14), pcol(15), 10.5, LT, p8, MUL)
    ts(r("pf", 5, 6), pcol(14), 0.125, MUL)
    lomask = r("pf", 5, 6)
    for j, c in enumerate((0, 9, 10, 11, 4, 8, 5, 12)):
        ts(r("tmpd", 32 * j, 32 * j + 32), r("cod", 0, 32), float(c), ADD, p_, EQ)
    cp(r("RW", 0, 32), r("tmpd", 0, 32))
    tt(r("RW", 3, 32, 4), r("tmpd", 35, 64, 4), r("tmpd", 67, 96, 4), ADD)
    tt(r("RW", 3, 32, 4), r("RW", 3, 32, 4), r("tmpd", 99, 128, 4), ADD)
    tt(r("RW", 32, 64), r("tmpd", 128, 160), r("tmpd", 160, 192), ADD)
    tt(r("tmpd", 0, 32), r("tmpd", 192, 224), r("tmpd", 32, 64), ADD)
    tt(r("RW", 64, 96), r("RW", 32, 64), r("tmpd", 0, 32), SUB)
    cp(r("RW", 67, 96, 4), r("RW", 35, 64, 4))
    tt(r("RW", 35, 64, 4), r("tmpd", 227, 256, 4), r("tmpd", 131, 160, 4), SUB)
    act(r("ulut"), r("iob", 0, 64), ACT.Identity, -1.0 / 64, r("ONF", 0, 1))
    ms(r("RM"), 1.0)
    ms(r("RM", 0, 64, 4), 0.0)
    ms(r("cb", 0, 528, 264), 0.0)
    ms(r("Z1", 4096, 4112), 256.0)
    ms(r("xw", 0, 8), 0.0)
    ts(r("WL"), r("WL"), pf, EQ)
    ts(r("WL", 1, 32, 2), r("WL", 1, 32, 2), 4096.0, MUL)
    ts(pcol(17), pm, 3.0, NE)
    ts(pcol(18), p12, 0.25, MUL)
    ts(pcol(19), pm, 3.0, EQ, 16.0, MUL)
    ts(r("offf", 0, 4), r("offf", 0, 4), pcol(18), ADD, pcol(17), MUL)
    ts(r("offc", 0, 4), r("offf", 0, 4), pcol(19), ADD)
    ts(r("offc", 4, 16), r("offf", 4, 16), p12, ADD)
    ts(pcol(20), p8, 3.0, MUL, p7, ADD)
    ts(r("offc", 16, 22), r("offf", 16, 22), pcol(20), ADD)
    ts(r("sm", 0, 64), r("sm", 0, 64), pf, ADD)
    act(r("th", 4, 5), r("ONF", 0, 1), ACT.Exp, -1.0)
    ts(r("elut"), r("elut"), r("th", 4, 5), MUL)
    tt(r("elut"), r("elut"), r("t96", 0, 48), SUB)

    for t in range(2):
        for a in range(8):
            dma("sa"[a % 2] if t == 0 else "s", "d%d" % (5 + t), r("nxw", 1024 * t, 1024 * t + 1024, p=(16 * a, 16 * a + 16)),
                landed("li", T.li[4 * t:4 * t + 4]), 3.0)
    dma("s", "d7", r("hu", 0, 64), landed("lh", T.lh[:, 0:64, :]))
    dma("a", "d8", r("hu", 64, 128), landed("lh", T.lh[:, 64:128, :]))
    dma("s", "d22", r("hu", 128, 192), landed("li", T.li[:, 96:128, :]))
    late[8] = 0
    for q in range(4, 8):
        dma("s", "d23", (T.dz[:, 1024 * q - 4096:1024 * q - 3072], [("dz", 0, 1)]),
            T.z[g0:g1, :] if q == me else (T.lz[q], [("lz", q, q + 1)]), 2.3, () if q == me else group["d6"])
    for a in range(8):
        dma("s", "d24", r("Z1", 0, 4096, p=(16 * a, 16 * a + 16)), whole("dz"), 4.4)
    for q in sorted([q for q in range(4) if late[q] < 2], key=lambda q: late[q]):
        for a in range(8):
            dma("sa"[a % 2], "d4", r("Z0", 1024 * q, 1024 * q + 1024, p=(16 * a, 16 * a + 16)),
                T.z[g0:g1, :] if q == me else (T.lz[q], [("lz", q, q + 1)]), 3.2)
    for i, q in enumerate([8] + [q for q in range(4) if late[q] == 2]):
        pa, pb = (("P0", "P1"), ("P2", "P3"), ("P6", "P7"))[i % 3]
        for ch in range(8):
            mm(r((pa, pb)[ch // 4], 128 * (ch % 4), 128 * (ch % 4) + 128), r("REP", 128 * ch, 128 * ch + 128),
               r("zl", 128 * q, 128 * q + 128))
        c = 1024 * (q if q < 4 else 4)
        (cp if late[q] == 2 else act)(r("Z0", c, c + 512), r(pa))
        act(r("Z0", c + 512, c + 1024), r(pb))

    part[0] = 1
    tt(r("G0"), ind(r("nxw", 0, 1024), r("uc0", 0, 16)), r("mk1", 0, 256), MUL)
    mm(r("P4", 16, 40), r("G0", 0, 128), r("SEL"))
    mm(r("P4", 40, 64), r("G0", 128, 256), r("SEL"))
    cp(r("uh", 0, 64), r("hu", 0, 64))
    cp(r("uh", 64, 128), r("hu", 64, 128))
    ts(r("ti", 0, 64), r("hu", 0, 64), 3, SHR)
    ts(r("ti", 64, 128), r("hu", 0, 64), 7, AND)
    cp(r("tfb"), r("ti", 0, 64))
    ts(r("tf", 128, 192), r("ti", 64, 128), 4.0, MUL, 4096.0, ADD)
    cp(r("uz"), r("P4", 16, 40))
    cp(r("ni", 8, 32), r("P4", 16, 40))
    cp(r("ni", 40, 64), r("P4", 40, 64))
    tt(r("d0g"), ind(r("Z0", 0, 4096), r("uz")), r("xg"), SUB)
    act(r("ab", 0, 384), r("d0g"), ACT.Abs)
    act(r("dq"), r("d0g"), scale=0.25)
    ts(r("nb", 0, 64), r("ni"), 1023, AND)
    ts(r("nb", 64, 128), r("ni"), 10, SHR)
    cp(r("ucb"), r("nb"))
    ts(r("near", 0, 384), r("ab", 0, 384), 1.0, LE_)
    act(r("tm", 0, 128), r("G0", 128, 256))
    tt(r("tm", 128, 256), r("G0", 128, 256), r("tm", 0, 128), SUB)
    for j in range(2):
        mm(r("P4", 256, 384), r("LE", 768 + 128 * j, 896 + 128 * j), r("tm", 128 * j, 128 * j + 128), j == 0, False)
    mm(r("P4", 256, 384), r("CR", 0, 128, p=(0, 1)), r("iob", p=(0, 1)), False, False)
    mm(r("P4", 256, 384), r("CR", 512, 640, p=(0, 1)), r("ONE", 0, 128, p=(0, 1)), False, False)
    for m in range(3):
        mm(r("P4", 256, 384), r("LW", 128 * m, 128 * m + 128), r("near", 128 * m, 128 * m + 128), False, m == 2)
    cp(r("tb", 0, 128), r("P4", 256, 384))
    for q in range(8):
        mm(r("P%d" % (q // 4), 128 * (q % 4), 128 * (q % 4) + 128), r("RQ", 128 * q, 128 * q + 128), r("tb", 0, 128))
    cp(r("tab0", 0, 512), r("P0"))
    act(r("tab0", 512, 1024), r("P1"))
    for k in range(4):
        act(r("fe", 256 * k, 256 * k + 256), ind(r("tab0"), r("uh", 16 * k, 16 * k + 16)))

    def fields(h):
        for u in range(4 * h, 4 * h + 4):
            for w in range(3):
                c = 128 * w + 32 * (u % 4)
                mm(r("P%d" % (2 + h), c, c + 32), r("fe", 128 * u, 128 * u + 128), r("RW", 32 * w, 32 * w + 32))

    def evac(t, h):
        o = 256 * t + 128 * h
        pb = "P%d" % (2 + h)
        ts(r("V", o, o + 128), r(pb, 0, 128), -4.0, ADD, 0.0, MAX)
        if t == 0:
            cp(r("PAT", o + 3, o + 128, 4), r(pb, 3, 128, 4))
            cp(r("ti", 128 + 32 * h, 160 + 32 * h), r(pb, 3, 128, 4))
            ms(r("V", o + 3, o + 128, 4), 2.0)
        else:
            cp(r("uo0", 32 * h, 32 * h + 32), r(pb, 3, 128, 4))
            tt(r("tf", 64 + 32 * h, 96 + 32 * h), r(pb, 131, 256, 4), r("tf", 128 + 32 * h, 160 + 32 * h), ADD)
        act(r("D", o, o + 128), r(pb, 256, 384))
        act(r("N", o, o + 128), r(pb, 128, 256))
    for h in range(2):
        fields(h)
        evac(0, h)
    ts(r("ti", 192, 256), r("ti", 128, 192), 7, AND)
    ts(r("PAT", 259, 512, 4), r("ti", 192, 256), 4.0, MUL)
    for h in range(2):
        act(r("ue", 512 * h, 512 * h + 512), ind(r("ulut"), r("uh", 64 + 32 * h, 96 + 32 * h)))
    for u in range(8):
        mm(r("P5", 8 * u, 8 * u + 8), r("ue", 128 * u, 128 * u + 128), r("R8"))
    act(r("ub", 0, 64), r("P5", 0, 64))
    for c in range(64):
        ts(r("A", 128 * c, 128 * c + 128), r("iob"), r("tfb", c, c + 1), EQ)

    part[0] = 2
    for m in range(4):
        if m % 2 == 0:
            a, b = 512 + 128 * m, 768 + 128 * m
            act(r("mk1", a, b), ind(r("MB"), r("ucb", 96 + 8 * m, 112 + 8 * m)))
            tt(r("G1", a, b), ind(r("nxw", 1024, 2048), r("ucb", 32 + 8 * m, 48 + 8 * m)), r("mk1", a, b), MUL)
        mm(r("P6", 24 * m, 24 + 24 * m), r("G1", 512 + 128 * m, 640 + 128 * m), r("SEL"))
    act(r("t96"), r("P6", 0, 96))
    cp(r("uz1"), ind(r("t96"), r("offc", 16, 22)))
    tt(r("xn", 128, 512), r("P5", 128, 512), r("dq"), ADD)
    act(r("mk1", 0, 512), ind(r("MB"), r("ucb", 64, 96)))
    tt(r("G1", 0, 512), ind(r("nxw", 1024, 2048), r("ucb", 0, 32)), r("mk1", 0, 512), MUL)
    mm(r("P7"), r("CR", 256, 384, p=(0, 1)), r("ONE", 0, 512, p=(0, 1)), True, False)
    mm(r("P7"), r("CR", 640, 768, p=(0, 1)), r("mrow", p=(0, 1)), False, False)
    mm(r("P7", 0, 128), r("CR", 128, 256, p=(0, 1)), r("iob", p=(0, 1)), False, False)
    mm(r("P7", 0, 128), r("CR", 384, 512, p=(0, 1)), r("ONE", 0, 128, p=(0, 1)), False, False)
    for m in range(3):
        for j in range(2):
            mm(r("P7", 128 * m + 128, 128 * m + 256), r("LE", 384 * j + 128 * m, 384 * j + 128 * m + 128),
               r("tm", 128 * j, 128 * j + 128), False, False)
    for m in range(4):
        mm(r("P7", 128 * m, 128 * m + 128), r("LN"), r("G1", 128 * m, 128 * m + 128), False, False)
    for a, b in ((0, 512), (512, 1024), (1024, 1280), (1280, 1536)):
        m, c = a // 512, a % 512
        tt(r("d1g", a, b), ind(r("Z1", 0, 4096), r("uz1", a // 16, b // 16)), r("xn", c, c + b - a), SUB)
        act(r("ab", a, b), r("d1g", a, b), ACT.Abs)
        ts(r("near", a, b), r("ab", a, b), 1.0, LE_)
        mm(r("P7", c, c + b - a), r("LW", 128 * m, 128 * m + 128), r("near", a, b), False, b == 1536)
    act(r("tm"), r("P7"), scale=lomask)
    tt(r("tb"), r("P7"), r("tm"), SUB)
    for q in range(8):
        dma("sa"[q % 2], "d9", whole("dt", T.dt[:, 512 * q:512 * q + 512]), r("tb", p=(16 * q, 16 * q + 16)), 2.4)
    for a in range(8):
        dma("sa"[a % 2], "d10", r("tab1", p=(16 * a, 16 * a + 16)), whole("dt"), 4.4)

    def draw(t, k):
        o = 256 * t + 64 * k
        c = 264 * t + 64 * k
        scan(r("R", o, o + 64), r("RM"), r("V", o, o + 64))
        w = 128 * t + 32 * k
        tt(r("tt", w, w + 16), r("R", o + 3, o + 64, 4), r("ub", 64 * t + 16 * k, 64 * t + 16 * k + 16), MUL)
        tt(r("cb", c + 1, c + 65), ind(r("tt", w, w + 24), r("offc", 0, 4)), r("R", o, o + 64), LE_)
        if t == 1 or k < 3:
            scan(r("TK", o, o + 64), r("cb", c, c + 64), r("D", o, o + 64))
        if k < 3:
            n = 64 * (3 - k)
            tt(r("ne", 0, n), ind(r("TK", o, o + 64), r("offc", 4, 4 + n // 16)), r("N", o + 64, o + 64 + n), NE)
            tt(r("V", o + 64, o + 128), r("V", o + 64, o + 128), r("ne", 0, 64), MUL)
            if k < 2:
                tt(r("V", o + 128, o + 64 + n), r("V", o + 128, o + 64 + n), r("ne", 64, n), MUL)
        return r("cb", c, c + 64)

    part[0] = 3
    for k in range(4):
        c = draw(0, k)
        scan(r("O0", 128 * k, 128 * k + 64), c, r("PAT", 64 * k, 64 * k + 64))
        scan(r("O0", 128 * k + 64, 128 * k + 128), c, r("PAT", 256 + 64 * k, 320 + 64 * k))
        cp(r("uo1", 32 * k, 32 * k + 32), r("O0", 128 * k + 3, 128 * k + 128, 4))
        act(r("mE", 256 * k, 256 * k + 256), ind(r("WL"), r("uo1", 32 * k + 16, 32 * k + 32)))
        pb = "P%d" % (k % 2)
        for j in range(2):
            mm(r(pb, 128 * j, 128 * j + 128), r("mE", 256 * k + 128 * j, 256 * k + 128 * j + 128), r("IQ", 0, 128))
        act(r("Bm", 256 * k, 256 * k + 256), r(pb, 0, 256))
        for c in range(16 * k, 16 * k + 16):
            mm(r("P6", 16 * k, 16 * k + 16), r("A", 128 * c, 128 * c + 128), r("Bm", 16 * c, 16 * c + 16), c % 16 == 0, c % 16 == 15)
    red(r("ecol", 0, 1), r("cb", 3, 256, 4))
    d = (me - 1) % 8
    to = T.cores[d] if d in direct else rl[d]
    rid, pid = topo.addr(to, core)
    ee = topo.engines(core, to)
    if d in direct:
        sent = remote(lambda: g.remote_dma(T.ein[:, 0:1], T.ecol[:, 0:1], S.win, S.loc, pid, rid, emask(ee)), len(ee), [r("ecol")])
    else:
        sent = remote(lambda: g.remote_dma(T.rw[:], T.ecol[:, 0:1], S.r2, S.loc, pid, rid, emask(ee)), len(ee), [r("ecol")])
    part[0] = 4
    q = (me + 1) % 8
    arrive("win", len(topo.engines(T.cores[q] if me in plans[q][0] else plans[q][2][me], core)), r("ein"), 5.5, [sent])
    for k in range(4):
        (cp if k % 2 else act)(r("fe", 256 * k, 256 * k + 256), ind(r("tab1"), r("uo1", 32 * k, 32 * k + 16)))
    for h in range(2):
        fields(h)
        evac(1, h)
        act(r("xr", 512 * h, 512 * h + 512), ind(r("Z0", 4096, 5120), r("uh", 32 * h, 32 * h + 32)))
        act(r("zr", 512 * h, 512 * h + 512), ind(r("Z0"), r("uo0", 32 * h, 32 * h + 32)))
    ts(r("tf", 192, 256), r("tfb"), 32.0, MUL)
    tt(r("tf", 192, 256), r("tf", 192, 256), r("tf", 64, 128), ADD)
    act(r("tf", 64, 128), r("tf", 64, 128), scale=4.0)
    ts(r("ub", 64, 128), r("hu", 128, 192), -1.0 / 64, MUL, 1.0, ADD)
    ts(r("sm", 128, 192), r("N", 259, 512, 4), -4096.0, EQ, 8.0, MUL)

    def theta(src, n, t):
        ts(r("mk", 0, n), src, 0.5, GT)
        scan(r("inc", 0, n), r("ONE", 0, n), r("mk", 0, n))
        mm(r("P7", 0, 1), r("TRI"), r("inc", n - 1, n))
        ts(r("cmp", 0, n), r("inc", 0, n), r("P7", 0, 1), ADD, 1024.5, LT)
        mm(r("P7", 128, 128 + n), r("ONE", 0, 128), r("cmp", 0, n))
        red(r("th", t, t + 1), r("P7", 128, 128 + n))
    cp(r("ni"), r("P6", 0, 64))
    ts(r("nb", 0, 128, 2), r("ni"), 4095, AND)
    ts(r("nb", 1, 128, 2), r("ni"), 12, SHR)
    tt(r("sm", 512, 576), r("nb", 0, 64), r("nb", 64, 128), ADD)
    tt(r("sm", 576, 608), r("sm", 512, 544), r("sm", 544, 576), ADD)
    theta(r("sm", 576, 608), 32, 0)
    mm(r("P4", 0, 1), r("ONF"), r("ein", 0, 1))
    ts(r("ti", 0, 1), r("P4", 0, 1), -1.0, MUL, 9216.0, ADD)
    ts(r("ti", 1, 2), r("ti", 0, 1), 10, SHR)
    cp(r("th", 2, 3), r("ti", 1, 2))
    ts(r("V", 259, 512, 4), r("V", 259, 512, 4), 0.0, MUL, r("th", 2, 3), ADD)
    ts(r("sm", 192, 256), r("tf", 192, 256), r("th", 0, 1), GE)
    tt(r("ub", 64, 128), r("ub", 64, 128), r("sm", 192, 256), MAX)
    ts(r("sm", 256, 320), r("tf", 192, 256), r("th", 0, 1), GE, 100000.0, MUL)
    tt(r("PAT", 515, 768, 4), r("sm", 256, 320), r("tf", 64, 128), ADD)

    for h in range(2):
        a, b = 512 * h, 512 * h + 512
        mm(r("P%d" % h), r("IQ", 384, 512), r("xr", a, b), True, False)
        mm(r("P%d" % h), r("IQ", 256, 384), r("zr", a, b), False, True)
        act(r("xw", 8 + a, 8 + b), r("P%d" % h))
    for h in range(2):
        a, b = 512 * h, 512 * h + 512
        mm(r("P%d" % (4 + h)), r("IQ", 128, 256), r("xr", a, b), True, False)
        mm(r("P%d" % (4 + h)), r("IQ", 0, 128), r("zr", a, b), False, True)
        act(r("G1", a, b), r("P%d" % (4 + h)), ACT.Abs)
        act(r("ex0", a, b), r("G1", a, b), ACT.Exp, -1.0)
    dma("g", "d14", r("ex0", 0, 512), r("ex0", 512, 1024), 3.5, accum_op=ADD)
    dma("g", "d15", r("ex0", 0, 256), r("ex0", 256, 512), 3.0, accum_op=ADD)

    part[0] = 5
    for k in range(4):
        c = draw(1, k)
        scan(r("O1", 64 * k, 64 * k + 64), c, r("PAT", 512 + 64 * k, 576 + 64 * k))
        cp(r("ut1", 16 * k, 16 * k + 16), r("TK", 256 + 64 * k + 3, 256 + 64 * k + 64, 4))
        for c in range(16 * k, 16 * k + 16):
            if c % 16 < 14:
                ts(r("Bm", 128 * c, 128 * c + 128), r("iob"), r("O1", 4 * c + 3, 4 * c + 4), EQ)
            else:
                act(r("ab", 128 * (c % 8), 128 * (c % 8) + 128), r("iob"), ACT.Abs, -1.0, r("O1", 4 * c + 3, 4 * c + 4))
                act(r("Bm", 128 * c, 128 * c + 128), r("ab", 128 * (c % 8), 128 * (c % 8) + 128), ACT.Relu, -1.0, r("ONF", 0, 1))
            mm(r("P6", 0, 128), r("A", 128 * c, 128 * c + 128), r("Bm", 128 * c, 128 * c + 128), c == 0, c == 63)
        a, b = 256 * k, 256 * k + 256
        act(r("ue", a, b), ind(r("Z1"), r("ut1", 16 * k, 16 * k + 16)))
        tt(r("d1", a, b), r("ue", a, b), r("P%d" % (k // 2), 256 * (k % 2), 256 * (k % 2) + 256), SUB)
        act(r("x1q", a, b), r("d1", a, b), scale=0.25)
        act(r("ad", a, b), r("d1", a, b), ACT.Abs)
        act(r("P%d" % (2 + k), 0, 256), r("ad", a, b), ACT.Exp, -1.0)
        tt(r("xw", 1032 + a, 1032 + b), r("P%d" % (k // 2), 256 * (k % 2), 256 * (k % 2) + 256), r("x1q", a, b), ADD)
    part[0] = 6
    hit = r("cb", 264 + 3, 264 + 256, 4)
    act(r("tf", 256, 320), r("tfb"), scale=128.0)
    tt(r("tf", 256, 320), r("tf", 256, 320), r("O1", 3, 256, 4), ADD)
    act(r("tf", 320, 384), hit, scale=1024.0)
    tt(r("tf", 320, 384), r("tf", 320, 384), r("sm", 0, 64), ADD)
    tt(r("sm", 320, 384), hit, r("sm", 192, 256), MAX)
    tt(r("sm", 320, 384), r("sm", 128, 192), r("sm", 320, 384), SUB)
    tt(r("sm", 384, 416), r("sm", 320, 352), r("sm", 352, 384), ADD)
    tt(r("sm", 416, 432), r("sm", 384, 400), r("sm", 400, 416), ADD)
    ts(r("uf", 64, 80), r("sm", 416, 432), 4.0, ADD)
    tt(r("ye_s"), ind(r("elut"), r("uf", 64, 80)), r("ex0", 0, 256), ADD)
    for k in range(4):
        tt(r("ye_s"), r("P%d" % (2 + k), 0, 256), r("ye_s"), ADD)
    theta(r("P6", 0, 128), 128, 1)
    ts(r("sm", 448, 512), r("tf", 256, 320), r("th", 1, 2), LT)
    tt(r("sm", 448, 512), r("sm", 448, 512), r("tf", 320, 384), MUL)
    cp(r("uf", 0, 64), r("sm", 448, 512))
    act(r("d1", 0, 256), ind(r("xw"), r("uf", 0, 16)))
    cp(r("d1", 256, 512), ind(r("xw"), r("uf", 16, 32)))
    tt(r("d1", 512, 768), ind(r("xw"), r("uf", 32, 48)), r("d1", 256, 512), ADD)
    tt(r("d1", 768, 1024), ind(r("xw"), r("uf", 48, 64)), r("d1", 0, 256), ADD)
    tt(r("yx_s"), r("d1", 512, 768), r("d1", 768, 1024), ADD)

    for i, (src, st, ld, rb, sr, so, out) in enumerate((("ye_s", "se", "le", "re_", "r3", "oe", T.ye),
                                                        ("yx_s", "sx", "lx", "rx", "r4", "ox", T.yx))):
        dma("s", "d%d" % (16 + 3 * i), whole(st), r(src))
        dma("a", "d%d" % (17 + 3 * i), whole(ld, T[ld][me]), r(src, p=(g0, g1)))
        tr_ = [xfer(topo, core, T.cores[d], eo[2 * j:2 * j + 2], S[so], T[st][d], T[ld][me]) for j, d in enumerate(direct)]
        tr_ += [xfer(topo, core, rl[d], rest[2 * j:2 * j + 2], S[sr], T[st][d], T[rb][:])
                for j, d in enumerate([d for d in rl if d not in direct])]
        sent = remote(lambda tr_=tr_: g.remote_dma_fused(tr_, local_sem=S.loc), 2 * len(tr_), [whole(st)])
        arrive(so, nout, (None, [(ld, 1, 2)]), 5.0, [sent])
        dma("sa"[i], "d%d" % (18 + 3 * i), out[:], whole(ld))

    n = len(ops)
    succ = [[] for _ in range(n)]
    for i, o in enumerate(ops):
        for j in o[6]:
            succ[j].append(i)
    prio = [0.0] * n
    for i in range(n - 1, -1, -1):
        prio[i] = ops[i][5] + AHEAD.get("^" + ops[i][7], 0.0) + max([prio[j] for j in succ[i]] + [0.0])
    prio = [x + AHEAD.get(o[7], 0.0) for x, o in zip(prio, ops)]
    left = [len(o[6]) for o in ops]
    ready = [0.0] * n
    free = {e: 0.0 for e in list(Q) + ["x"]}
    cand = {e: [] for e in free}
    for i in range(n):
        if not left[i]:
            cand[ops[i][0]].append(i)
    cnt = {}
    val = [0] * n
    known = {e: {} for e in Q}
    for _ in range(n):
        i = min((j for c in cand.values() for j in c), key=lambda j: int(ORDER[2 * j:2 * j + 2], 36))
        t0 = 0.0
        cand[ops[i][0]].remove(i)
        e, fn, sem, inc, busy, lat, pre = ops[i][:7]
        t0 = max(t0, ready[i])
        free[e] = t0 + busy
        for j in succ[i]:
            ready[j] = max(ready[j], t0 + (lat if ops[j][6][i] or ops[j][0] == "x" else busy))
            left[j] -= 1
            if not left[j]:
                cand[ops[j][0]].append(j)
        if e != "x":
            need = {}
            for j, w in pre.items():
                if w and ops[j][2] != "loc":
                    need[ops[j][2]] = max(need.get(ops[j][2], 0), val[j])
            for s2, v2 in need.items():
                if known[e].get(s2, 0) < v2:
                    Q[e].wait_ge(S[s2], v2)
                    known[e][s2] = v2
            call = fn()
            if inc > 0:
                call.then_inc(S[sem], inc)
        cnt[sem] = cnt.get(sem, 0) + abs(inc)
        val[i] = cnt[sem]
    for s2, v2 in cnt.items():
        if known["g"].get(s2, 0) < v2:
            g.wait_ge(S[s2], v2)
